import numpy as np
import ml_dtypes


def mxq(x, axis, fmt="e4m3"):
    dtype, down = {"e4m3": (ml_dtypes.float8_e4m3fn, 7), "e5m2": (ml_dtypes.float8_e5m2, 14)}[fmt]
    v = np.moveaxis(np.asarray(x, np.float32).astype(ml_dtypes.bfloat16).astype(np.float64), axis, -1)
    blocks = v.reshape(v.shape[:-1] + (-1, 32))
    amax = np.abs(blocks).max(-1, keepdims=True)
    byte = np.maximum(np.where(amax > 0, np.frexp(amax)[1] - 1 + 127, 0) - down, 1)
    scale = np.exp2(byte - 127.0)
    codes = (blocks / scale).astype(np.float32).astype(dtype).astype(np.float64)
    return np.moveaxis((codes * scale).reshape(v.shape), -1, axis)


WIDE = False


def mx_kscale(k):
    if not WIDE:
        return np.ones(k)
    levels = np.array([10, -10, 5, -5, 0])
    if k % 512:
        return np.exp2(np.random.permutation(np.resize(levels, k // 32))).repeat(32)
    a = np.empty((k // 512, 16))
    for p in range(k // 512):
        a[p, :8] = np.random.permutation(np.resize(levels, 8))
        for g in range(8):
            far = levels[np.abs(levels - a[p, g]) >= 10]
            a[p, g + 8] = far[np.random.randint(len(far))]
    return np.exp2(a.ravel()).repeat(32)


BF16 = ml_dtypes.bfloat16


def bf(x):
    return np.asarray(x, np.float32).astype(BF16)


def f64(x):
    return np.asarray(x).astype(np.float64)

E4M3FN = np.array([(-1.0 if i & 128 else 1.0) * ((1.0 + (i & 7) / 8.0) * 2.0 ** (((i >> 3) & 15) - 7) if i & 120 else (i & 7) * 2.0 ** -9) for i in range(256)])


def e4m3fn_bytes(y):
    return np.clip(np.asarray(y, np.float64), -448.0, 448.0).astype(np.float32).astype(ml_dtypes.float8_e4m3fn).view(np.uint8)


def e4m3fn_values(b):
    return E4M3FN[b]

def planes(Y):
    n, m = Y.shape
    b = f64(bf(Y)).reshape(n // 32, 32, m)
    amax = np.abs(b).max(1)
    byte = np.clip(np.where(amax > 0, np.frexp(amax)[1] - 1 + 127 - 7, 1), 1, 254)
    codes = (b * np.exp2(127.0 - byte)[:, None, :]).reshape(n, m).astype(np.float32).astype(ml_dtypes.float8_e4m3fn).view(np.uint8)
    words = codes.reshape(n // 512, 128, 4, m).transpose(0, 1, 3, 2)
    return np.ascontiguousarray(words), np.ascontiguousarray(byte.astype(np.uint8).reshape(n // 512, 16, m))


T, K, N = 2048, 1536, 1024

def setup_inputs():
    s = mx_kscale(K)
    spread = np.exp(0.5 * np.random.randn(1, K))
    X = np.random.randn(T, K) * spread * s[None, :]
    X_scale = (np.abs(X).max(axis=0, keepdims=True) / 448.0).astype(np.float32)
    X_bytes = e4m3fn_bytes(X / f64(X_scale))
    mean = bf(0.5 * np.random.randn(1, K) * s[None, :])
    B = bf(0.35 * np.random.randn(K, N) / np.sqrt(K) / s[:, None])
    H0 = bf(np.exp(np.linspace(-1.9, 0.9, N)[None, :] + 0.2 * np.random.randn(1, N)))
    frailty = bf(np.exp(0.4 * np.random.randn(T, 1)))
    return {"X_bytes": X_bytes, "X_scale": X_scale, "mean": mean,
            "B": B, "H0": H0, "frailty": frailty}

def reference(X_bytes, X_scale, mean, B, H0, frailty):
    X = e4m3fn_values(X_bytes) * f64(X_scale) + f64(mean)
    eta = mxq(X, 1) @ mxq(f64(B), 0)
    H = np.exp(eta) * f64(H0) * f64(frailty)
    y = np.exp(-H)
    Y = y.T
    words, scales = planes(Y)
    return y, words, scales

@@ -1,0 +1,278 @@
+from contextlib import ExitStack
+
+import concourse.mybir as mybir
+from concourse.masks import make_identity
+
+T, K, N = 2048, 1536, 1024
+FLOPS = 2 * T * K * N
+
+F32 = mybir.dt.float32
+BF16 = mybir.dt.bfloat16
+U32 = mybir.dt.uint32
+I32 = mybir.dt.int32
+U8 = mybir.dt.uint8
+FP8 = mybir.dt.float8_e4m3fn
+FP8X4 = mybir.dt.float8_e4m3fn_x4
+ALU = mybir.AluOpType
+ACT = mybir.ActivationFunctionType
+
+P = 128
+W = 512
+PASSES = K // W
+GROUPS = T // W
+HALVES = N // W
+UNITS = GROUPS * HALVES
+SLABS = 2 * UNITS
+
+
+def tile_cox_frailty_survival_b15_kernel(tc, X_bytes, X_scale, mean, B, H0, frailty, out_0, out_1, out_2):
+    nc = tc.nc
+    with ExitStack() as ctx:
+        keep = ctx.enter_context(tc.tile_pool(name="keep", bufs=1))
+        work = ctx.enter_context(tc.tile_pool(name="work", bufs=2))
+        psum = ctx.enter_context(tc.psum_pool(name="psum", bufs=2))
+        ctx.enter_context(tc.manual_schedule())
+
+        rows = keep.tile([P, P], BF16, name="rows")
+        nc.gpsimd.memset(rows[:], 0.0)
+        ones = keep.tile([P, 1], F32, name="ones")
+        nc.gpsimd.memset(ones[:], 1.0)
+        ident16 = keep.tile([P, P], BF16, name="ident16")
+        make_identity(nc, ident16[:])
+        ident32 = keep.tile([P, P], F32, name="ident32")
+        make_identity(nc, ident32[:])
+
+        scale = keep.tile([P, PASSES, 4], F32, name="scale")
+        mean16 = keep.tile([P, PASSES, 4], BF16, name="mean16")
+        nc.scalar.dma_start(out=rows[0:8, :], in_=H0.rearrange("o (j p) -> (o j) p", p=P))
+        nc.scalar.dma_start(out=rows[8:24, :], in_=frailty.rearrange("(i p) o -> i (p o)", p=P))
+        nc.scalar.dma_start(out=scale[:], in_=X_scale.rearrange("o (g p t) -> p (o g) t", p=P, t=4))
+        nc.scalar.dma_start(out=mean16[:], in_=mean.rearrange("o (g p t) -> p (o g) t", p=P, t=4))
+
+        xbytes = {}
+        braw = {}
+
+        def load_x(c):
+            G, g = divmod(c, PASSES)
+            xbytes[c] = keep.tile([P, 4, W], U8, name="xbytes%d" % c)
+            src = X_bytes[G * W : (G + 1) * W, g * W : (g + 1) * W]
+            nc.sync.dma_start(out=xbytes[c][:], in_=src.rearrange("(i p) k -> p i k", p=P))
+
+        def load_b(b):
+            h, g = divmod(b, PASSES)
+            braw[b] = work.tile([P, 4, W], BF16, name="braw%d" % b, tag="slab", bufs=SLABS)
+            src = B[g * W : (g + 1) * W, h * W : (h + 1) * W]
+            nc.sync.dma_start(out=braw[b][:], in_=src.rearrange("(p t) n -> p t n", t=4))
+
+        for g in range(PASSES):
+            load_x(g)
+            load_b(g)
+        for g in range(PASSES):
+            load_x(PASSES + g)
+            load_b(PASSES + g)
+        for c in range(2 * PASSES, GROUPS * PASSES):
+            load_x(c)
+
+        cols = psum.tile([P, P], BF16, name="cols", tag="ybank")
+        nc.tensor.transpose(cols[:], rows[:], ident16[:])
+        log_h0 = keep.tile([P, 8], F32, name="log_h0")
+        nc.scalar.activation(out=log_h0[:], in_=cols[:, 0:8], func=ACT.Ln)
+        neg_f = keep.tile([P, 16], F32, name="neg_f")
+        nc.scalar.activation(out=neg_f[:], in_=cols[:, 8:24], func=ACT.Copy, scale=-1.0)
+        mean32 = keep.tile([P, PASSES, 4], F32, name="mean32")
+        nc.scalar.copy(out=mean32[:], in_=mean16[:])
+
+        wide, xbank, planes, woven = {}, {}, {}, {}
+        xcodes, xscales, bcodes, bscales = {}, {}, {}, {}
+        acc, hazard, ebank, y, y16, ybank, ywoven = {}, {}, {}, {}, {}, {}, {}
+        yscales = {}
+
+        def widen(c):
+            wide[c] = work.tile([P, 2, W, 2], BF16, name="wide")
+            src = xbytes[c][:].rearrange("p i k -> p (i k)").bitcast(FP8)
+            nc.vector.tensor_scalar(
+                out=wide[c][:].rearrange("p u n e -> p n u e"),
+                in0=src.rearrange("p (n u e) -> p n u e", u=2, e=2),
+                scalar1=ones[:], scalar2=None, op0=ALU.mult)
+
+        def turn_x(c, u):
+            words = wide[c][:].rearrange("p u n e -> p (u n e)").bitcast(F32)
+            xbank[c, u] = psum.tile([P, W], F32, name="xbank")
+            for i in range(4):
+                nc.tensor.transpose(xbank[c, u][:, i * P : (i + 1) * P], words[:, u * W + i * P : u * W + (i + 1) * P], ident32[:])
+
+        def affine(c, u):
+            g = c % PASSES
+            if u == 0:
+                planes[c] = work.tile([P, 4, W], BF16, name="planes", bufs=3)
+            pairs = xbank[c, u][:].bitcast(BF16).rearrange("p (n e) -> p e n", e=2)
+            for e in range(2):
+                t = 2 * u + e
+                if (lambda c,u,e: c>2 and c%3!=0 and u==1)(c, u, e):
+                    nc.vector.tensor_scalar(out=planes[c][:, t, :], in0=pairs[:, e, :], scalar1=scale[:, g, t : t + 1],
+                                            scalar2=mean32[:, g, t : t + 1], op0=ALU.mult, op1=ALU.add)
+                else:
+                    nc.scalar.activation(out=planes[c][:, t, :], in_=pairs[:, e, :], func=ACT.Identity,
+                                         scale=scale[:, g, t : t + 1], bias=mean32[:, g, t : t + 1])
+
+        def weave(key, src, copy):
+            woven[key] = work.tile([P, W, 4], BF16, name="woven", bufs=3, align_bytes=64)
+            copy(out=woven[key][:].rearrange("p (c i) t -> p c t i", i=4), in_=src[:].rearrange("p t (c i) -> p c t i", i=4))
+
+        def quantise(key, codes, scales, label):
+            codes[key[1]] = keep.tile([P, W], U32, name="%scodes%d" % (label, key[1]), align_bytes=64)
+            scales[key[1]] = keep.tile([P, W], U8, name="%sscales%d" % (label, key[1]), align_bytes=64)
+            nc.vector.quantize_mx(out=codes[key[1]][:].bitcast(FP8X4), scales=scales[key[1]][:],
+                                  in_=woven[key][:].rearrange("p n t -> p (n t)"))
+
+        def product(unit, j):
+            G, h = divmod(unit, HALVES)
+            acc[unit, j] = psum.tile([P, W], F32, name="acc")
+            for g in range(PASSES):
+                b, c = h * PASSES + g, G * PASSES + g
+                nc.tensor.matmul_mx(out=acc[unit, j][:], lhsT=bcodes[b][:, j * P : (j + 1) * P].bitcast(FP8X4),
+                                    lhsT_scale=bscales[b][:, j * P : (j + 1) * P], rhs=xcodes[c][:].bitcast(FP8X4),
+                                    rhs_scale=xscales[c][:], start=(g == 0), stop=(g == PASSES - 1))
+
+        def first_exp(unit, j):
+            col = (unit % HALVES) * 4 + j
+            hazard[unit, j] = work.tile([P, W], F32, name="hazard", bufs=8)
+            nc.scalar.activation(out=hazard[unit, j][:], in_=acc[unit, j][:], func=ACT.Exp, bias=log_h0[:, col : col + 1])
+
+        def turn_e(unit, i):
+            ebank[unit, i] = psum.tile([P, W], F32, name="ebank")
+            for j in range(4):
+                nc.tensor.transpose(ebank[unit, i][:, j * P : (j + 1) * P], hazard[unit, j][:, i * P : (i + 1) * P], ident32[:])
+
+        def second_exp(slab, r):
+            unit, half = divmod(slab, 2)
+            G, h = divmod(unit, HALVES)
+            if r == 0:
+                y[slab] = work.tile([P, 2, W], F32, name="y", tag="slab", bufs=SLABS)
+            col = G * 4 + 2 * half + r
+            nc.scalar.activation(out=y[slab][:, r, :], in_=ebank[unit, 2 * half + r][:], func=ACT.Exp, scale=neg_f[:, col : col + 1])
+            if r == 1:
+                dst = out_0[(col - 1) * P : (col + 1) * P, h * W : (h + 1) * W]
+                nc.sync.dma_start(out=dst.rearrange("(i p) n -> p i n", p=P), in_=y[slab][:])
+
+        def round_y(slab):
+            y16[slab] = work.tile([P, 2, 2 * P, 2], BF16, name="y16", bufs=3)
+            nc.vector.tensor_copy(out=y16[slab][:], in_=y[slab][:].rearrange("p i (q u e) -> p u (i q) e", u=2, e=2))
+
+        def turn_y(slab):
+            words = y16[slab][:].rearrange("p u n e -> p (u n e)").bitcast(F32)
+            ybank[slab] = psum.tile([P, W], F32, name="ybank")
+            for q in range(4):
+                nc.tensor.transpose(ybank[slab][:, q * P : (q + 1) * P], words[:, q * P : (q + 1) * P], ident32[:])
+
+        def empty_y(slab):
+            ywoven[slab] = work.tile([P, 2 * P, 2], F32, name="ywoven", bufs=3, align_bytes=64)
+            copy = nc.scalar.copy if (lambda s: s>=10 and s%2==1)(slab) else nc.vector.tensor_copy
+            copy(out=ywoven[slab][:], in_=ybank[slab][:].rearrange("p (u m) -> p m u", u=2))
+
+        def quantise_y(slab):
+            unit, half = divmod(slab, 2)
+            G, h = divmod(unit, HALVES)
+            if slab % 4 == 0:
+                yscales[G] = work.tile([P, HALVES, W], U8, name="yscales", align_bytes=64)
+            ycodes = work.tile([P, 2 * P], U32, name="ycodes", bufs=4, align_bytes=64)
+            nc.vector.quantize_mx(out=ycodes[:].bitcast(FP8X4), scales=yscales[G][:, h, half * 2 * P : (half + 1) * 2 * P],
+                                  in_=ywoven[slab][:].rearrange("p m u -> p (m u)").bitcast(BF16))
+            words = out_1[h].rearrange("p m t -> p (m t)").bitcast(I32)
+            at = G * W + half * 2 * P
+            nc.sync.dma_start(out=words[:, at : at + 2 * P], in_=ycodes[:].bitcast(I32))
+            if slab % 4 == 3:
+                for q in range(4):
+                    dst = out_2[:, 4 * q : 4 * q + 4, G * W : (G + 1) * W].rearrange("h r m -> r h m").bitcast(I32)
+                    nc.sync.dma_start(out=dst, in_=yscales[G][32 * q : 32 * q + 4, :, :].bitcast(I32))
+
+        def weave_b(b, copy):
+            weave(("b", b), braw[b], copy)
+
+        def quantise_b(b):
+            quantise(("b", b), bcodes, bscales, "b")
+
+        def weave_x(c):
+            weave(("x", c), planes[c], nc.vector.tensor_copy)
+
+        def quantise_x(c):
+            quantise(("x", c), xcodes, xscales, "x")
+
+        def turn_and_affine(c):
+            for u in range(2):
+                turn_x(c, u)
+                affine(c, u)
+
+        widen(0)
+        turn_and_affine(0)
+        weave_b(0, nc.vector.tensor_copy)
+        widen(1)
+        turn_and_affine(1)
+        quantise_b(0)
+        widen(2)
+        turn_and_affine(2)
+        weave_x(0)
+        weave_b(1, nc.vector.tensor_copy)
+        quantise_x(0)
+        quantise_b(1)
+        weave_x(1)
+        weave_b(2, nc.scalar.copy)
+        widen(3)
+        quantise_x(1)
+        weave_x(2)
+        quantise_b(2)
+        quantise_x(2)
+
+        def halves_at(step):
+            return [divmod(n + 2 * PASSES, 2) for n in range(2 * PASSES * (GROUPS - 1)) if (2 * n) // 3 + (-1) == step]
+
+        y_at = {8: [0], 10: [1], 11: [2, 3], 12: [4, 5], 13: [6, 7], 14: [8, 9], 15: [10, 11], 16: [12, 13], 17: [14], 18: [15]}
+        for step in range(-1, 21):
+            unit, half = divmod(step, 2)
+            mult = 0 <= step < SLABS
+            back = 0 <= step - 2 < SLABS
+            xs = halves_at(step)
+            done = [c for c, u in halves_at(step - 1) if u == 1]
+            ahead = [c for c, u in halves_at(step + 1) if u == 0 and c > PASSES]
+            ys = y_at.get(step, [])
+            if mult:
+                product(unit, 2 * half)
+                product(unit, 2 * half + 1)
+            for s in ys:
+                round_y(s)
+            for c in ahead:
+                widen(c)
+            if step == 0:
+                weave_b(3, nc.vector.tensor_copy)
+            if step == 1:
+                weave_b(5, nc.vector.tensor_copy)
+            for s in y_at.get(step - 1, []):
+                quantise_y(s)
+            for c in done:
+                weave_x(c)
+            if step == 0:
+                quantise_b(3)
+            if step == 1:
+                quantise_b(4)
+                quantise_b(5)
+            for r in range(2):
+                if back:
+                    turn_e(unit - 1, 2 * half + r)
+                if r < len(xs):
+                    turn_x(*xs[r])
+                if r < len(ys):
+                    turn_y(ys[r])
+            if mult:
+                first_exp(unit, 2 * half)
+                first_exp(unit, 2 * half + 1)
+            if step == 0:
+                weave_b(4, nc.scalar.copy)
+            for c in done:
+                quantise_x(c)
+            for r in range(2):
+                if back:
+                    second_exp(step - 2, r)
+                if r < len(xs):
+                    affine(*xs[r])
+                if r < len(ys):
+                    empty_y(ys[r])

@@ -18,11 +18,12 @@ ACT = mybir.ActivationFunctionType
 
 P = 128
 W = 512
+S = 256
 PASSES = K // W
-GROUPS = T // W
 HALVES = N // W
-UNITS = GROUPS * HALVES
-SLABS = 2 * UNITS
+SLABS = HALVES * T // S
+WIDTHS = (512, 512, 512, 512)
+STARTS = tuple(sum(WIDTHS[:G]) for G in range(len(WIDTHS)))
 
 
 def tile_cox_frailty_survival_b15_kernel(tc, X_bytes, X_scale, mean, B, H0, frailty, out_0, out_1, out_2):
@@ -42,36 +43,39 @@ def tile_cox_frailty_survival_b15_kernel(tc, X_bytes, X_scale, mean, B, H0, frai
         ident32 = keep.tile([P, P], F32, name="ident32")
         make_identity(nc, ident32[:])
 
-        scale = keep.tile([P, PASSES, 4], F32, name="scale")
-        mean16 = keep.tile([P, PASSES, 4], BF16, name="mean16")
-        nc.scalar.dma_start(out=rows[0:8, :], in_=H0.rearrange("o (j p) -> (o j) p", p=P))
-        nc.scalar.dma_start(out=rows[8:24, :], in_=frailty.rearrange("(i p) o -> i (p o)", p=P))
-        nc.scalar.dma_start(out=scale[:], in_=X_scale.rearrange("o (g p t) -> p (o g) t", p=P, t=4))
-        nc.scalar.dma_start(out=mean16[:], in_=mean.rearrange("o (g p t) -> p (o g) t", p=P, t=4))
-
         xbytes = {}
         braw = {}
 
-        def load_x(c):
-            G, g = divmod(c, PASSES)
-            xbytes[c] = keep.tile([P, 4, W], U8, name="xbytes%d" % c)
-            src = X_bytes[G * W : (G + 1) * W, g * W : (g + 1) * W]
-            nc.sync.dma_start(out=xbytes[c][:], in_=src.rearrange("(i p) k -> p i k", p=P))
+        def load_x(G, g):
+            xbytes[G, g] = keep.tile([P, WIDTHS[G] // P, W], U8, name="xbytes%d_%d" % (G, g))
+            src = X_bytes[STARTS[G] : STARTS[G] + WIDTHS[G], g * W : (g + 1) * W]
+            nc.sync.dma_start(out=xbytes[G, g][:], in_=src.rearrange("(i p) k -> p i k", p=P))
 
-        def load_b(b):
-            h, g = divmod(b, PASSES)
-            braw[b] = work.tile([P, 4, W], BF16, name="braw%d" % b, tag="slab", bufs=SLABS)
+        def load_b(h, g):
+            braw[h, g] = work.tile([P, 4, W], BF16, name="braw", tag="slab", bufs=SLABS)
             src = B[g * W : (g + 1) * W, h * W : (h + 1) * W]
-            nc.sync.dma_start(out=braw[b][:], in_=src.rearrange("(p t) n -> p t n", t=4))
+            nc.sync.dma_start(out=braw[h, g][:], in_=src.rearrange("(p t) n -> p t n", t=4))
 
+        scale = keep.tile([P, PASSES, 4], F32, name="scale")
+        mean16 = keep.tile([P, PASSES, 4], BF16, name="mean16")
+        nc.scalar.dma_start(out=scale[:], in_=X_scale.rearrange("o (g p t) -> p (o g) t", p=P, t=4))
+        nc.scalar.dma_start(out=mean16[:], in_=mean.rearrange("o (g p t) -> p (o g) t", p=P, t=4))
+        nc.scalar.dma_start(out=rows[0:8, :], in_=H0.rearrange("o (j p) -> (o j) p", p=P))
+        nc.scalar.dma_start(out=rows[8:24, :], in_=frailty.rearrange("(i p) o -> i (p o)", p=P))
+        load_x(0, 0)
+        load_b(0, 0)
+        load_x(0, 1)
+        load_x(0, 2)
+        load_b(0, 1)
+        load_b(0, 2)
+        load_x(1, 0)
+        load_x(1, 1)
         for g in range(PASSES):
-            load_x(g)
-            load_b(g)
-        for g in range(PASSES):
-            load_x(PASSES + g)
-            load_b(PASSES + g)
-        for c in range(2 * PASSES, GROUPS * PASSES):
-            load_x(c)
+            load_b(1, g)
+        load_x(1, 2)
+        for G in range(2, len(WIDTHS)):
+            for g in range(PASSES):
+                load_x(G, g)
 
         cols = psum.tile([P, P], BF16, name="cols", tag="ybank")
         nc.tensor.transpose(cols[:], rows[:], ident16[:])
@@ -79,84 +83,113 @@ def tile_cox_frailty_survival_b15_kernel(tc, X_bytes, X_scale, mean, B, H0, frai
         nc.scalar.activation(out=log_h0[:], in_=cols[:, 0:8], func=ACT.Ln)
         neg_f = keep.tile([P, 16], F32, name="neg_f")
         nc.scalar.activation(out=neg_f[:], in_=cols[:, 8:24], func=ACT.Copy, scale=-1.0)
+
         mean32 = keep.tile([P, PASSES, 4], F32, name="mean32")
         nc.scalar.copy(out=mean32[:], in_=mean16[:])
+        wide, xbank, planes, woven, codes, scales = {}, {}, {}, {}, {}, {}
+        acc, hazard, ebank, y, y16, ybank, ywoven, yscales = {}, {}, {}, {}, {}, {}, {}, {}
+        quantised = []
+        on_vector = lambda G, g, u: G > 0 and u == 1
+        single = lambda G, g: G in (1, 2)
 
-        wide, xbank, planes, woven = {}, {}, {}, {}
-        xcodes, xscales, bcodes, bscales = {}, {}, {}, {}
-        acc, hazard, ebank, y, y16, ybank, ywoven = {}, {}, {}, {}, {}, {}, {}
-        yscales = {}
-
-        def widen(c):
-            wide[c] = work.tile([P, 2, W, 2], BF16, name="wide")
-            src = xbytes[c][:].rearrange("p i k -> p (i k)").bitcast(FP8)
+        def widen(G, g):
+            src = xbytes[G, g][:].rearrange("p i k -> p (i k)").bitcast(FP8)
+            run = 1 if single(G, g) else 2
+            wide[G, g] = work.tile([P, 4 // run, WIDTHS[G], run], BF16, name="wide", bufs=3)
             nc.vector.tensor_scalar(
-                out=wide[c][:].rearrange("p u n e -> p n u e"),
-                in0=src.rearrange("p (n u e) -> p n u e", u=2, e=2),
+                out=wide[G, g][:].rearrange("p u n e -> p n u e"),
+                in0=src.rearrange("p (n u e) -> p n u e", u=4 // run, e=run),
                 scalar1=ones[:], scalar2=None, op0=ALU.mult)
 
-        def turn_x(c, u):
-            words = wide[c][:].rearrange("p u n e -> p (u n e)").bitcast(F32)
-            xbank[c, u] = psum.tile([P, W], F32, name="xbank")
-            for i in range(4):
-                nc.tensor.transpose(xbank[c, u][:, i * P : (i + 1) * P], words[:, u * W + i * P : u * W + (i + 1) * P], ident32[:])
+        def turn_x(G, g, u):
+            width = WIDTHS[G]
+            flat = wide[G, g][:].rearrange("p u n e -> p (u n e)")
+            if single(G, g):
+                xbank[G, g, u] = psum.tile([P, 2 * width], BF16, name="xbank")
+                src, ident, count = flat[:, 2 * u * width : 2 * (u + 1) * width], ident16, 2 * width // P
+            else:
+                xbank[G, g, u] = psum.tile([P, width], F32, name="xbank")
+                src, ident, count = flat.bitcast(F32)[:, u * width : (u + 1) * width], ident32, width // P
+            for i in range(count):
+                nc.tensor.transpose(xbank[G, g, u][:, i * P : (i + 1) * P], src[:, i * P : (i + 1) * P], ident[:])
 
-        def affine(c, u):
-            g = c % PASSES
+        def affine(G, g, u):
+            width = WIDTHS[G]
             if u == 0:
-                planes[c] = work.tile([P, 4, W], BF16, name="planes", bufs=3)
-            pairs = xbank[c, u][:].bitcast(BF16).rearrange("p (n e) -> p e n", e=2)
+                planes[G, g] = work.tile([P, 4, width], BF16, name="planes", bufs=3)
             for e in range(2):
                 t = 2 * u + e
-                if (lambda c,u,e: c>2 and c%3!=0 and u==1)(c, u, e):
-                    nc.vector.tensor_scalar(out=planes[c][:, t, :], in0=pairs[:, e, :], scalar1=scale[:, g, t : t + 1],
-                                            scalar2=mean32[:, g, t : t + 1], op0=ALU.mult, op1=ALU.add)
+                if single(G, g):
+                    src = xbank[G, g, u][:, e * width : (e + 1) * width]
                 else:
-                    nc.scalar.activation(out=planes[c][:, t, :], in_=pairs[:, e, :], func=ACT.Identity,
+                    src = xbank[G, g, u][:].bitcast(BF16).rearrange("p (n e) -> p e n", e=2)[:, e, :]
+                if on_vector(G, g, u):
+                    nc.vector.tensor_scalar(out=planes[G, g][:, t, :], in0=src,
+                                            scalar1=scale[:, g, t : t + 1], scalar2=mean32[:, g, t : t + 1], op0=ALU.mult, op1=ALU.add)
+                else:
+                    nc.scalar.activation(out=planes[G, g][:, t, :], in_=src, func=ACT.Identity,
                                          scale=scale[:, g, t : t + 1], bias=mean32[:, g, t : t + 1])
 
-        def weave(key, src, copy):
-            woven[key] = work.tile([P, W, 4], BF16, name="woven", bufs=3, align_bytes=64)
+        def weave(key, src, width, copy):
+            woven[key] = work.tile([P, width, 4], BF16, name="woven" + key[0], bufs=3 if key[0] == "x" else 4, align_bytes=64)
             copy(out=woven[key][:].rearrange("p (c i) t -> p c t i", i=4), in_=src[:].rearrange("p t (c i) -> p c t i", i=4))
 
-        def quantise(key, codes, scales, label):
-            codes[key[1]] = keep.tile([P, W], U32, name="%scodes%d" % (label, key[1]), align_bytes=64)
-            scales[key[1]] = keep.tile([P, W], U8, name="%sscales%d" % (label, key[1]), align_bytes=64)
-            nc.vector.quantize_mx(out=codes[key[1]][:].bitcast(FP8X4), scales=scales[key[1]][:],
+        def quantise(key, width):
+            codes[key] = keep.tile([P, width], U32, name="codes_%s%d_%d" % key, align_bytes=64)
+            scales[key] = keep.tile([P, width], U8, name="scales_%s%d_%d" % key, align_bytes=64)
+            nc.vector.quantize_mx(out=codes[key][:].bitcast(FP8X4), scales=scales[key][:],
                                   in_=woven[key][:].rearrange("p n t -> p (n t)"))
 
-        def product(unit, j):
-            G, h = divmod(unit, HALVES)
-            acc[unit, j] = psum.tile([P, W], F32, name="acc")
+        def weave_b(q, g):
+            weave(("b", q, g), braw[q // 2, g][:, :, (q % 2) * S : (q % 2 + 1) * S], S, nc.scalar.copy if (q, g) in ((0, 0), (1, 0), (1, 1), (2, 0), (2, 1), (3, 0), (3, 1)) else nc.vector.tensor_copy)
+
+        def quantise_b(q, g):
+            quantise(("b", q, g), S)
+
+        def weave_x(G, g):
+            weave(("x", G, g), planes[G, g], WIDTHS[G], nc.vector.tensor_copy)
+
+        def quantise_x(G, g):
+            quantise(("x", G, g), WIDTHS[G])
+
+        def product(G, h, j):
+            width = WIDTHS[G]
+            per_bank = W // width
+            if j % per_bank == 0:
+                acc[G, h, j // per_bank] = psum.tile([P, per_bank, width], F32, name="acc")
             for g in range(PASSES):
-                b, c = h * PASSES + g, G * PASSES + g
-                nc.tensor.matmul_mx(out=acc[unit, j][:], lhsT=bcodes[b][:, j * P : (j + 1) * P].bitcast(FP8X4),
-                                    lhsT_scale=bscales[b][:, j * P : (j + 1) * P], rhs=xcodes[c][:].bitcast(FP8X4),
-                                    rhs_scale=xscales[c][:], start=(g == 0), stop=(g == PASSES - 1))
+                nc.tensor.matmul_mx(out=acc[G, h, j // per_bank][:, j % per_bank, :],
+                                    lhsT=codes["b", 2 * h + j // 2, g][:, (j % 2) * P : (j % 2 + 1) * P].bitcast(FP8X4),
+                                    lhsT_scale=scales["b", 2 * h + j // 2, g][:, (j % 2) * P : (j % 2 + 1) * P], rhs=codes["x", G, g][:].bitcast(FP8X4),
+                                    rhs_scale=scales["x", G, g][:], start=(g == 0), stop=(g == PASSES - 1))
 
-        def first_exp(unit, j):
-            col = (unit % HALVES) * 4 + j
-            hazard[unit, j] = work.tile([P, W], F32, name="hazard", bufs=8)
-            nc.scalar.activation(out=hazard[unit, j][:], in_=acc[unit, j][:], func=ACT.Exp, bias=log_h0[:, col : col + 1])
+        def first_exp(G, h, j):
+            width = WIDTHS[G]
+            per_bank = W // width
+            hazard[G, h, j] = work.tile([P, width], F32, name="hazard", bufs=10)
+            nc.scalar.activation(out=hazard[G, h, j][:], in_=acc[G, h, j // per_bank][:, j % per_bank, :], func=ACT.Exp,
+                                 bias=log_h0[:, 4 * h + j : 4 * h + j + 1])
 
-        def turn_e(unit, i):
-            ebank[unit, i] = psum.tile([P, W], F32, name="ebank")
+        def turn_e(slab, r):
+            G, h, half = slab
+            ebank[slab, r] = psum.tile([P, W], F32, name="ebank", tag="acc" if slab == (len(WIDTHS) - 1, 1, 1) else "ebank")
+            i = 2 * half + r
             for j in range(4):
-                nc.tensor.transpose(ebank[unit, i][:, j * P : (j + 1) * P], hazard[unit, j][:, i * P : (i + 1) * P], ident32[:])
+                nc.tensor.transpose(ebank[slab, r][:, j * P : (j + 1) * P], hazard[G, h, j][:, i * P : (i + 1) * P], ident32[:])
 
         def second_exp(slab, r):
-            unit, half = divmod(slab, 2)
-            G, h = divmod(unit, HALVES)
+            G, h, half = slab
+            first = STARTS[G] + half * S
             if r == 0:
                 y[slab] = work.tile([P, 2, W], F32, name="y", tag="slab", bufs=SLABS)
-            col = G * 4 + 2 * half + r
-            nc.scalar.activation(out=y[slab][:, r, :], in_=ebank[unit, 2 * half + r][:], func=ACT.Exp, scale=neg_f[:, col : col + 1])
+            col = first // P + r
+            nc.scalar.activation(out=y[slab][:, r, :], in_=ebank[slab, r][:], func=ACT.Exp, scale=neg_f[:, col : col + 1])
             if r == 1:
-                dst = out_0[(col - 1) * P : (col + 1) * P, h * W : (h + 1) * W]
+                dst = out_0[first : first + S, h * W : (h + 1) * W]
                 nc.sync.dma_start(out=dst.rearrange("(i p) n -> p i n", p=P), in_=y[slab][:])
 
         def round_y(slab):
-            y16[slab] = work.tile([P, 2, 2 * P, 2], BF16, name="y16", bufs=3)
+            y16[slab] = work.tile([P, 2, S, 2], BF16, name="y16", bufs=3)
             nc.vector.tensor_copy(out=y16[slab][:], in_=y[slab][:].rearrange("p i (q u e) -> p u (i q) e", u=2, e=2))
 
         def turn_y(slab):
@@ -165,114 +198,135 @@ def tile_cox_frailty_survival_b15_kernel(tc, X_bytes, X_scale, mean, B, H0, frai
             for q in range(4):
                 nc.tensor.transpose(ybank[slab][:, q * P : (q + 1) * P], words[:, q * P : (q + 1) * P], ident32[:])
 
-        def empty_y(slab):
-            ywoven[slab] = work.tile([P, 2 * P, 2], F32, name="ywoven", bufs=3, align_bytes=64)
-            copy = nc.scalar.copy if (lambda s: s>=10 and s%2==1)(slab) else nc.vector.tensor_copy
+        def empty_y(slab, copy):
+            ywoven[slab] = work.tile([P, S, 2], F32, name="ywoven", bufs=5, align_bytes=64)
             copy(out=ywoven[slab][:], in_=ybank[slab][:].rearrange("p (u m) -> p m u", u=2))
 
         def quantise_y(slab):
-            unit, half = divmod(slab, 2)
-            G, h = divmod(unit, HALVES)
-            if slab % 4 == 0:
-                yscales[G] = work.tile([P, HALVES, W], U8, name="yscales", align_bytes=64)
-            ycodes = work.tile([P, 2 * P], U32, name="ycodes", bufs=4, align_bytes=64)
-            nc.vector.quantize_mx(out=ycodes[:].bitcast(FP8X4), scales=yscales[G][:, h, half * 2 * P : (half + 1) * 2 * P],
+            G, h, half = slab
+            first = STARTS[G] + half * S
+            if G not in yscales:
+                yscales[G] = work.tile([P, HALVES, WIDTHS[G]], U8, name="yscales", align_bytes=64)
+            ycodes = work.tile([P, S], U32, name="ycodes", bufs=4, align_bytes=64)
+            nc.vector.quantize_mx(out=ycodes[:].bitcast(FP8X4), scales=yscales[G][:, h, half * S : (half + 1) * S],
                                   in_=ywoven[slab][:].rearrange("p m u -> p (m u)").bitcast(BF16))
             words = out_1[h].rearrange("p m t -> p (m t)").bitcast(I32)
-            at = G * W + half * 2 * P
-            nc.sync.dma_start(out=words[:, at : at + 2 * P], in_=ycodes[:].bitcast(I32))
-            if slab % 4 == 3:
+            nc.sync.dma_start(out=words[:, first : first + S], in_=ycodes[:].bitcast(I32))
+            quantised.append(G)
+            if quantised.count(G) == HALVES * WIDTHS[G] // S:
                 for q in range(4):
-                    dst = out_2[:, 4 * q : 4 * q + 4, G * W : (G + 1) * W].rearrange("h r m -> r h m").bitcast(I32)
+                    dst = out_2[:, 4 * q : 4 * q + 4, STARTS[G] : STARTS[G] + WIDTHS[G]].rearrange("h r m -> r h m").bitcast(I32)
                     nc.sync.dma_start(out=dst, in_=yscales[G][32 * q : 32 * q + 4, :, :].bitcast(I32))
 
-        def weave_b(b, copy):
-            weave(("b", b), braw[b], copy)
+        def half_x(G, g, u):
+            turn_x(G, g, u)
+            affine(G, g, u)
 
-        def quantise_b(b):
-            quantise(("b", b), bcodes, bscales, "b")
+        widen(0, 0)
+        weave_b(0, 0)
+        half_x(0, 0, 0)
+        half_x(0, 0, 1)
+        widen(0, 1)
+        half_x(0, 1, 0)
+        half_x(0, 1, 1)
+        widen(0, 2)
+        quantise_b(0, 0)
+        half_x(0, 2, 0)
+        half_x(0, 2, 1)
+        weave_b(0, 1)
+        weave_x(0, 0)
+        quantise_b(0, 1)
+        weave_b(0, 2)
+        quantise_x(0, 0)
+        weave_x(0, 1)
+        quantise_b(0, 2)
+        weave_b(1, 0)
+        weave_b(1, 1)
+        weave_x(0, 2)
+        quantise_x(0, 1)
+        widen(1, 0)
+        quantise_x(0, 2)
 
-        def weave_x(c):
-            weave(("x", c), planes[c], nc.vector.tensor_copy)
-
-        def quantise_x(c):
-            quantise(("x", c), xcodes, xscales, "x")
-
-        def turn_and_affine(c):
-            for u in range(2):
-                turn_x(c, u)
-                affine(c, u)
-
-        widen(0)
-        turn_and_affine(0)
-        weave_b(0, nc.vector.tensor_copy)
-        widen(1)
-        turn_and_affine(1)
-        quantise_b(0)
-        widen(2)
-        turn_and_affine(2)
-        weave_x(0)
-        weave_b(1, nc.vector.tensor_copy)
-        quantise_x(0)
-        quantise_b(1)
-        weave_x(1)
-        weave_b(2, nc.scalar.copy)
-        widen(3)
-        quantise_x(1)
-        weave_x(2)
-        quantise_b(2)
-        quantise_x(2)
-
-        def halves_at(step):
-            return [divmod(n + 2 * PASSES, 2) for n in range(2 * PASSES * (GROUPS - 1)) if (2 * n) // 3 + (-1) == step]
-
-        y_at = {8: [0], 10: [1], 11: [2, 3], 12: [4, 5], 13: [6, 7], 14: [8, 9], 15: [10, 11], 16: [12, 13], 17: [14], 18: [15]}
-        for step in range(-1, 21):
-            unit, half = divmod(step, 2)
-            mult = 0 <= step < SLABS
-            back = 0 <= step - 2 < SLABS
-            xs = halves_at(step)
-            done = [c for c, u in halves_at(step - 1) if u == 1]
-            ahead = [c for c, u in halves_at(step + 1) if u == 0 and c > PASSES]
-            ys = y_at.get(step, [])
-            if mult:
-                product(unit, 2 * half)
-                product(unit, 2 * half + 1)
+        steps, slabs, ready = [], [], {}
+        for G, width in enumerate(WIDTHS):
+            for h in range(HALVES):
+                parts = width // S
+                for part in range(parts):
+                    steps.append([(G, h, j) for j in range(part * 4 // parts, (part + 1) * 4 // parts)])
+                for half in range(parts):
+                    slabs.append((G, h, half))
+                    ready.setdefault(min(len(steps) + half, 16), []).append((G, h, half))
+        x_at = {0: [(1,0,0),(1,0,1)], 1: [(1,1,0),(1,1,1)], 2: [(1,2,0),(1,2,1)], 3: [(2,0,0),(2,0,1)], 4: [(2,1,0),(2,1,1)], 5: [(2,2,0),(2,2,1)], 6: [(3,0,0)], 7: [(3,0,1)], 8: [(3,1,0)], 9: [(3,1,1)], 10: [(3,2,0),(3,2,1)]}
+        b_at = {-1: [(1, 0), (1, 1)], 0: [(1, 2), (2, 0), (2, 1)], 1: [(2, 2), (3, 0), (3, 1)], 2: [(3, 2)]}
+        y_at = {7: [0], 8: [1], 9: [2], 10: [3], 11: [4], 12: [5,6], 13: [7,8], 14: [9,10], 15: [11,12], 16: [13], 17: [14,15]}
+        ev_s = lambda step, r: step<12 or step>16
+        on_s = ((0, 0), (1, 0), (1, 1), (2, 0), (2, 1), (3, 0), (3, 1))
+        for step in range(0, 22):
+            products = steps[step] if 0 <= step < len(steps) else []
+            es = [(s, r) for s in ready.get(step, []) for r in range(2)]
+            xs = x_at.get(step, [])
+            done = [(G, g) for G, g, u in x_at.get(step - 2, []) if u == 1 and not on_vector(G, g, u)]
+            done = done + [(G, g) for G, g, u in x_at.get(step - 1, []) if u == 1 and on_vector(G, g, u)]
+            ahead = [(G, g) for G, g, u in x_at.get(step + 1, []) if u == 0 and (G, g) not in wide]
+            ys = [slabs[s] for s in y_at.get(step, [])]
+            before = list(enumerate(y_at.get(step - 1, [])))
+            late = [slabs[s] for r, s in enumerate(y_at.get(step - 2, [])) if ev_s(step - 2, r)]
+            late = late + [slabs[s] for r, s in before if not ev_s(step - 1, r)]
+            bs = b_at.get(step, [])
+            for m in products:
+                product(*m)
+            for x in x_at.get(step - 1, []):
+                if on_vector(*x):
+                    affine(*x)
+            for r, s in before:
+                if not ev_s(step - 1, r):
+                    empty_y(slabs[s], nc.vector.tensor_copy)
             for s in ys:
                 round_y(s)
             for c in ahead:
-                widen(c)
-            if step == 0:
-                weave_b(3, nc.vector.tensor_copy)
-            if step == 1:
-                weave_b(5, nc.vector.tensor_copy)
-            for s in y_at.get(step - 1, []):
-                quantise_y(s)
+                widen(*c)
+            for b in bs:
+                if b not in on_s:
+                    weave_b(*b)
             for c in done:
-                weave_x(c)
-            if step == 0:
-                quantise_b(3)
-            if step == 1:
-                quantise_b(4)
-                quantise_b(5)
+                weave_x(*c)
+            for b in b_at.get(step - 1, []):
+                if b in on_s:
+                    quantise_b(*b)
+            for b in bs:
+                if b not in on_s:
+                    quantise_b(*b)
+            for c in done:
+                quantise_x(*c)
+            for s in late:
+                quantise_y(s)
+
+            if len(es) > 2 and False:
+                for s in ys:
+                    turn_y(s)
             for r in range(2):
-                if back:
-                    turn_e(unit - 1, 2 * half + r)
+                if r < len(es):
+                    turn_e(*es[r])
                 if r < len(xs):
                     turn_x(*xs[r])
-                if r < len(ys):
-                    turn_y(ys[r])
-            if mult:
-                first_exp(unit, 2 * half)
-                first_exp(unit, 2 * half + 1)
-            if step == 0:
-                weave_b(4, nc.scalar.copy)
-            for c in done:
-                quantise_x(c)
-            for r in range(2):
-                if back:
-                    second_exp(step - 2, r)
-                if r < len(xs):
+            if len(es) <= 2:
+                for s in ys:
+                    turn_y(s)
+            for m in products:
+                first_exp(*m)
+            for r in range(max(len(es), 2)):
+                if r < len(es):
+                    second_exp(*es[r])
+                if r < len(xs) and not on_vector(*xs[r]):
                     affine(*xs[r])
-                if r < len(ys):
-                    empty_y(ys[r])
+                if r + 2 < len(es):
+                    turn_e(*es[r + 2])
+            if len(es) > 2 and not False:
+                for s in ys:
+                    turn_y(s)
+            for b in bs:
+                if b in on_s:
+                    weave_b(*b)
+            for r in range(len(ys)):
+                if ev_s(step, r):
+                    empty_y(ys[r], nc.scalar.copy)

@@ -90,11 +90,11 @@ def tile_cox_frailty_survival_b15_kernel(tc, X_bytes, X_scale, mean, B, H0, frai
         acc, hazard, ebank, y, y16, ybank, ywoven, yscales = {}, {}, {}, {}, {}, {}, {}, {}
         quantised = []
         on_vector = lambda G, g, u: G > 0 and u == 1
-        single = lambda G, g: G in (1, 2)
+        single = lambda G, g, u: G > 0 and u == 1
 
         def widen(G, g):
             src = xbytes[G, g][:].rearrange("p i k -> p (i k)").bitcast(FP8)
-            run = 1 if single(G, g) else 2
+            run = 2
             wide[G, g] = work.tile([P, 4 // run, WIDTHS[G], run], BF16, name="wide", bufs=3)
             nc.vector.tensor_scalar(
                 out=wide[G, g][:].rearrange("p u n e -> p n u e"),
@@ -103,15 +103,16 @@ def tile_cox_frailty_survival_b15_kernel(tc, X_bytes, X_scale, mean, B, H0, frai
 
         def turn_x(G, g, u):
             width = WIDTHS[G]
-            flat = wide[G, g][:].rearrange("p u n e -> p (u n e)")
-            if single(G, g):
+            if single(G, g, u):
                 xbank[G, g, u] = psum.tile([P, 2 * width], BF16, name="xbank")
-                src, ident, count = flat[:, 2 * u * width : 2 * (u + 1) * width], ident16, 2 * width // P
+                for e in range(2):
+                    for i in range(width // P):
+                        nc.tensor.transpose(xbank[G, g, u][:, e * width + i * P : e * width + (i + 1) * P], wide[G, g][:, u, i * P : (i + 1) * P, e], ident16[:])
             else:
                 xbank[G, g, u] = psum.tile([P, width], F32, name="xbank")
-                src, ident, count = flat.bitcast(F32)[:, u * width : (u + 1) * width], ident32, width // P
-            for i in range(count):
-                nc.tensor.transpose(xbank[G, g, u][:, i * P : (i + 1) * P], src[:, i * P : (i + 1) * P], ident[:])
+                src = wide[G, g][:].rearrange("p u n e -> p (u n e)").bitcast(F32)[:, u * width : (u + 1) * width]
+                for i in range(width // P):
+                    nc.tensor.transpose(xbank[G, g, u][:, i * P : (i + 1) * P], src[:, i * P : (i + 1) * P], ident32[:])
 
         def affine(G, g, u):
             width = WIDTHS[G]
@@ -119,7 +120,7 @@ def tile_cox_frailty_survival_b15_kernel(tc, X_bytes, X_scale, mean, B, H0, frai
                 planes[G, g] = work.tile([P, 4, width], BF16, name="planes", bufs=3)
             for e in range(2):
                 t = 2 * u + e
-                if single(G, g):
+                if single(G, g, u):
                     src = xbank[G, g, u][:, e * width : (e + 1) * width]
                 else:
                     src = xbank[G, g, u][:].bitcast(BF16).rearrange("p (n e) -> p e n", e=2)[:, e, :]
@@ -141,7 +142,7 @@ def tile_cox_frailty_survival_b15_kernel(tc, X_bytes, X_scale, mean, B, H0, frai
                                   in_=woven[key][:].rearrange("p n t -> p (n t)"))
 
         def weave_b(q, g):
-            weave(("b", q, g), braw[q // 2, g][:, :, (q % 2) * S : (q % 2 + 1) * S], S, nc.scalar.copy if (q, g) in ((0, 0), (1, 0), (1, 1), (2, 0), (2, 1), (3, 0), (3, 1)) else nc.vector.tensor_copy)
+            weave(("b", q, g), braw[q // 2, g][:, :, (q % 2) * S : (q % 2 + 1) * S], S, nc.scalar.copy if (q, g) in ((1, 0), (1, 1), (1, 2), (2, 0), (2, 1), (3, 0), (3, 1),) else nc.vector.tensor_copy)
 
         def quantise_b(q, g):
             quantise(("b", q, g), S)
@@ -152,30 +153,31 @@ def tile_cox_frailty_survival_b15_kernel(tc, X_bytes, X_scale, mean, B, H0, frai
         def quantise_x(G, g):
             quantise(("x", G, g), WIDTHS[G])
 
-        def product(G, h, j):
-            width = WIDTHS[G]
+        def product(G, h, j, first, width):
             per_bank = W // width
+            key = (G, h, j // per_bank, first)
             if j % per_bank == 0:
-                acc[G, h, j // per_bank] = psum.tile([P, per_bank, width], F32, name="acc")
+                acc[key] = psum.tile([P, per_bank, width], F32, name="acc")
             for g in range(PASSES):
-                nc.tensor.matmul_mx(out=acc[G, h, j // per_bank][:, j % per_bank, :],
+                nc.tensor.matmul_mx(out=acc[key][:, j % per_bank, :],
                                     lhsT=codes["b", 2 * h + j // 2, g][:, (j % 2) * P : (j % 2 + 1) * P].bitcast(FP8X4),
-                                    lhsT_scale=scales["b", 2 * h + j // 2, g][:, (j % 2) * P : (j % 2 + 1) * P], rhs=codes["x", G, g][:].bitcast(FP8X4),
-                                    rhs_scale=scales["x", G, g][:], start=(g == 0), stop=(g == PASSES - 1))
+                                    lhsT_scale=scales["b", 2 * h + j // 2, g][:, (j % 2) * P : (j % 2 + 1) * P],
+                                    rhs=codes["x", G, g][:, first : first + width].bitcast(FP8X4),
+                                    rhs_scale=scales["x", G, g][:, first : first + width], start=(g == 0), stop=(g == PASSES - 1))
 
-        def first_exp(G, h, j):
-            width = WIDTHS[G]
+        def first_exp(G, h, j, first, width):
             per_bank = W // width
-            hazard[G, h, j] = work.tile([P, width], F32, name="hazard", bufs=10)
-            nc.scalar.activation(out=hazard[G, h, j][:], in_=acc[G, h, j // per_bank][:, j % per_bank, :], func=ACT.Exp,
+            tile = work.tile([P, width], F32, name="hazard", bufs=10)
+            for i in range(width // P):
+                hazard[G, h, j, first // P + i] = tile[:, i * P : (i + 1) * P]
+            nc.scalar.activation(out=tile[:], in_=acc[G, h, j // per_bank, first][:, j % per_bank, :], func=ACT.Exp,
                                  bias=log_h0[:, 4 * h + j : 4 * h + j + 1])
 
         def turn_e(slab, r):
             G, h, half = slab
             ebank[slab, r] = psum.tile([P, W], F32, name="ebank", tag="acc" if slab == (len(WIDTHS) - 1, 1, 1) else "ebank")
-            i = 2 * half + r
             for j in range(4):
-                nc.tensor.transpose(ebank[slab, r][:, j * P : (j + 1) * P], hazard[G, h, j][:, i * P : (i + 1) * P], ident32[:])
+                nc.tensor.transpose(ebank[slab, r][:, j * P : (j + 1) * P], hazard[G, h, j, 2 * half + r], ident32[:])
 
         def second_exp(slab, r):
             G, h, half = slab
@@ -223,44 +225,51 @@ def tile_cox_frailty_survival_b15_kernel(tc, X_bytes, X_scale, mean, B, H0, frai
             affine(G, g, u)
 
         widen(0, 0)
-        weave_b(0, 0)
         half_x(0, 0, 0)
         half_x(0, 0, 1)
+        weave_b(0, 0)
         widen(0, 1)
         half_x(0, 1, 0)
         half_x(0, 1, 1)
-        widen(0, 2)
         quantise_b(0, 0)
+        widen(0, 2)
         half_x(0, 2, 0)
         half_x(0, 2, 1)
-        weave_b(0, 1)
         weave_x(0, 0)
-        quantise_b(0, 1)
-        weave_b(0, 2)
+        weave_b(0, 1)
         quantise_x(0, 0)
+        quantise_b(0, 1)
         weave_x(0, 1)
-        quantise_b(0, 2)
-        weave_b(1, 0)
-        weave_b(1, 1)
-        weave_x(0, 2)
+        weave_b(0, 2)
         quantise_x(0, 1)
-        widen(1, 0)
+        weave_x(0, 2)
+        quantise_b(0, 2)
+        for g in range(PASSES):
+            if (1, g) in ((1, 0), (1, 1), (1, 2), (2, 0), (2, 1), (3, 0), (3, 1),):
+                weave_b(1, g)
         quantise_x(0, 2)
+        widen(1, 0)
 
         steps, slabs, ready = [], [], {}
         for G, width in enumerate(WIDTHS):
             for h in range(HALVES):
                 parts = width // S
-                for part in range(parts):
-                    steps.append([(G, h, j) for j in range(part * 4 // parts, (part + 1) * 4 // parts)])
-                for half in range(parts):
-                    slabs.append((G, h, half))
-                    ready.setdefault(min(len(steps) + half, 16), []).append((G, h, half))
+                if 2 * G + h >= 8 - 0:
+                    for half in range(parts):
+                        steps.append([(G, h, j, half * S, S) for j in range(4)])
+                        slabs.append((G, h, half))
+                        ready.setdefault(len(steps), []).append((G, h, half))
+                else:
+                    for part in range(parts):
+                        steps.append([(G, h, j, 0, width) for j in range(part * 4 // parts, (part + 1) * 4 // parts)])
+                    for half in range(parts):
+                        slabs.append((G, h, half))
+                        ready.setdefault(min(len(steps) + half, 16), []).append((G, h, half))
         x_at = {0: [(1,0,0),(1,0,1)], 1: [(1,1,0),(1,1,1)], 2: [(1,2,0),(1,2,1)], 3: [(2,0,0),(2,0,1)], 4: [(2,1,0),(2,1,1)], 5: [(2,2,0),(2,2,1)], 6: [(3,0,0)], 7: [(3,0,1)], 8: [(3,1,0)], 9: [(3,1,1)], 10: [(3,2,0),(3,2,1)]}
-        b_at = {-1: [(1, 0), (1, 1)], 0: [(1, 2), (2, 0), (2, 1)], 1: [(2, 2), (3, 0), (3, 1)], 2: [(3, 2)]}
+        b_at = {0: [(2, 0), (2, 1)], 1: [(2, 2), (3, 0), (3, 1)], 2: [(3, 2)], -1: [(1, 0), (1, 1), (1, 2)]}
         y_at = {7: [0], 8: [1], 9: [2], 10: [3], 11: [4], 12: [5,6], 13: [7,8], 14: [9,10], 15: [11,12], 16: [13], 17: [14,15]}
-        ev_s = lambda step, r: step<12 or step>16
-        on_s = ((0, 0), (1, 0), (1, 1), (2, 0), (2, 1), (3, 0), (3, 1))
+        ev_s = lambda step, r: step<12 or step>15
+        on_s = ((1, 0), (1, 1), (1, 2), (2, 0), (2, 1), (3, 0), (3, 1),)
         for step in range(0, 22):
             products = steps[step] if 0 <= step < len(steps) else []
             es = [(s, r) for s in ready.get(step, []) for r in range(2)]

@@ -17,13 +17,22 @@ ALU = mybir.AluOpType
 ACT = mybir.ActivationFunctionType
 
 P = 128
-W = 512
-S = 256
-PASSES = K // W
-HALVES = N // W
-SLABS = HALVES * T // S
-WIDTHS = (512, 512, 512, 512)
-STARTS = tuple(sum(WIDTHS[:G]) for G in range(len(WIDTHS)))
+PACK = 4
+WIDE = 512
+NARROW = 256
+PASSES = K // WIDE
+GROUPS = T // WIDE
+SIDES = N // WIDE
+TILES = WIDE // P
+ROUNDS = GROUPS * SIDES
+BLOCKS = ROUNDS * TILES
+BANKS = 8
+SLABS = tuple((b, 2) for b in range(0, BLOCKS - 2, 2)) + ((BLOCKS - 2, 1), (BLOCKS - 1, 1))
+
+PIECES_ON_SCALAR = 2
+LAG = 2
+PLANES_FROM = 3
+PLANES_MOST = 4
 
 
 def tile_cox_frailty_survival_b15_kernel(tc, X_bytes, X_scale, mean, B, H0, frailty, out_0, out_1, out_2):
@@ -31,8 +40,11 @@ def tile_cox_frailty_survival_b15_kernel(tc, X_bytes, X_scale, mean, B, H0, frai
     with ExitStack() as ctx:
         keep = ctx.enter_context(tc.tile_pool(name="keep", bufs=1))
         work = ctx.enter_context(tc.tile_pool(name="work", bufs=2))
-        psum = ctx.enter_context(tc.psum_pool(name="psum", bufs=2))
+        psum = ctx.enter_context(tc.psum_pool(name="psum", bufs=BANKS))
         ctx.enter_context(tc.manual_schedule())
+
+        def bank(shape, dtype):
+            return psum.tile(shape, dtype, name="bank")
 
         rows = keep.tile([P, P], BF16, name="rows")
         nc.gpsimd.memset(rows[:], 0.0)
@@ -43,26 +55,27 @@ def tile_cox_frailty_survival_b15_kernel(tc, X_bytes, X_scale, mean, B, H0, frai
         ident32 = keep.tile([P, P], F32, name="ident32")
         make_identity(nc, ident32[:])
 
-        xbytes = {}
-        braw = {}
+        h0_rows, f_rows = slice(0, N // P), slice(N // P, N // P + T // P)
+        scale = keep.tile([P, PASSES, PACK], F32, name="scale")
+        mean16 = keep.tile([P, PASSES, PACK], BF16, name="mean16")
+        nc.scalar.dma_start(out=scale[:], in_=X_scale.rearrange("o (g p t) -> p (o g) t", p=P, t=PACK))
+        nc.scalar.dma_start(out=mean16[:], in_=mean.rearrange("o (g p t) -> p (o g) t", p=P, t=PACK))
 
-        def load_x(G, g):
-            xbytes[G, g] = keep.tile([P, WIDTHS[G] // P, W], U8, name="xbytes%d_%d" % (G, g))
-            src = X_bytes[STARTS[G] : STARTS[G] + WIDTHS[G], g * W : (g + 1) * W]
-            nc.sync.dma_start(out=xbytes[G, g][:], in_=src.rearrange("(i p) k -> p i k", p=P))
+        xbytes, braw = {}, {}
 
-        def load_b(h, g):
-            braw[h, g] = work.tile([P, 4, W], BF16, name="braw", tag="slab", bufs=SLABS)
-            src = B[g * W : (g + 1) * W, h * W : (h + 1) * W]
-            nc.sync.dma_start(out=braw[h, g][:], in_=src.rearrange("(p t) n -> p t n", t=4))
+        def load_x(group, g):
+            xbytes[group, g] = keep.tile([P, TILES, WIDE], U8, name="xbytes%d_%d" % (group, g))
+            src = X_bytes[group * WIDE : (group + 1) * WIDE, g * WIDE : (g + 1) * WIDE]
+            nc.sync.dma_start(out=xbytes[group, g][:], in_=src.rearrange("(i p) k -> p i k", p=P))
 
-        scale = keep.tile([P, PASSES, 4], F32, name="scale")
-        mean16 = keep.tile([P, PASSES, 4], BF16, name="mean16")
-        nc.scalar.dma_start(out=scale[:], in_=X_scale.rearrange("o (g p t) -> p (o g) t", p=P, t=4))
-        nc.scalar.dma_start(out=mean16[:], in_=mean.rearrange("o (g p t) -> p (o g) t", p=P, t=4))
-        nc.scalar.dma_start(out=rows[0:8, :], in_=H0.rearrange("o (j p) -> (o j) p", p=P))
-        nc.scalar.dma_start(out=rows[8:24, :], in_=frailty.rearrange("(i p) o -> i (p o)", p=P))
+        def load_b(side, g):
+            braw[side, g] = work.tile([P, PACK, WIDE], BF16, name="braw", tag="slab", bufs=BLOCKS // 2)
+            src = B[g * WIDE : (g + 1) * WIDE, side * WIDE : (side + 1) * WIDE]
+            nc.sync.dma_start(out=braw[side, g][:], in_=src.rearrange("(p t) n -> p t n", t=PACK))
+
         load_x(0, 0)
+        nc.sync.dma_start(out=rows[h0_rows, :], in_=H0.rearrange("o (j p) -> (o j) p", p=P))
+        nc.sync.dma_start(out=rows[f_rows, :], in_=frailty.rearrange("(i p) o -> i (p o)", p=P))
         load_b(0, 0)
         load_x(0, 1)
         load_x(0, 2)
@@ -73,67 +86,76 @@ def tile_cox_frailty_survival_b15_kernel(tc, X_bytes, X_scale, mean, B, H0, frai
         for g in range(PASSES):
             load_b(1, g)
         load_x(1, 2)
-        for G in range(2, len(WIDTHS)):
+        for group in range(2, GROUPS):
             for g in range(PASSES):
-                load_x(G, g)
+                load_x(group, g)
 
-        cols = psum.tile([P, P], BF16, name="cols", tag="ybank")
+        cols = bank([P, P], BF16)
         nc.tensor.transpose(cols[:], rows[:], ident16[:])
-        log_h0 = keep.tile([P, 8], F32, name="log_h0")
-        nc.scalar.activation(out=log_h0[:], in_=cols[:, 0:8], func=ACT.Ln)
-        neg_f = keep.tile([P, 16], F32, name="neg_f")
-        nc.scalar.activation(out=neg_f[:], in_=cols[:, 8:24], func=ACT.Copy, scale=-1.0)
-
-        mean32 = keep.tile([P, PASSES, 4], F32, name="mean32")
+        log_h0 = keep.tile([P, N // P], F32, name="log_h0")
+        nc.scalar.activation(out=log_h0[:], in_=cols[:, h0_rows], func=ACT.Ln)
+        warm = keep.tile([P, 1], F32, name="warm")
+        nc.scalar.activation(out=warm[:], in_=ones[:], func=ACT.Exp)
+        neg_f = keep.tile([P, T // P], F32, name="neg_f")
+        nc.scalar.activation(out=neg_f[:], in_=cols[:, f_rows], func=ACT.Copy, scale=-1.0)
+        mean32 = keep.tile([P, PASSES, PACK], F32, name="mean32")
         nc.scalar.copy(out=mean32[:], in_=mean16[:])
-        wide, xbank, planes, woven, codes, scales = {}, {}, {}, {}, {}, {}
-        acc, hazard, ebank, y, y16, ybank, ywoven, yscales = {}, {}, {}, {}, {}, {}, {}, {}
-        quantised = []
-        on_vector = lambda G, g, u: G > 0 and u == 1
-        single = lambda G, g, u: G > 0 and u == 1
 
-        def widen(G, g):
-            src = xbytes[G, g][:].rearrange("p i k -> p (i k)").bitcast(FP8)
-            run = 2
-            wide[G, g] = work.tile([P, 4 // run, WIDTHS[G], run], BF16, name="wide", bufs=3)
+        wide, xbank, xrows, woven, codes, scales = {}, {}, {}, {}, {}, {}
+        hazard, y, y16, ywoven, ycodes = {}, {}, {}, {}, {}
+        yscales = [keep.tile([P, SIDES, T // 2], U8, name="yscales%d" % half, align_bytes=64) for half in range(2)]
+
+        def window_of(group, g):
+            return 2 * group - 3 + min(g, 1)
+
+        last_x_window = window_of(GROUPS - 1, PASSES - 1)
+
+        def on_vector(group, u):
+            return group > 0 and u == 1
+
+        def as_bf16(group, g, u):
+            return on_vector(group, u) and window_of(group, g) < last_x_window
+
+        def widen(group, g):
+            wide[group, g] = work.tile([P, 2, WIDE, 2], BF16, name="wide", bufs=3)
+            src = xbytes[group, g][:].rearrange("p i k -> p (i k)").bitcast(FP8)
             nc.vector.tensor_scalar(
-                out=wide[G, g][:].rearrange("p u n e -> p n u e"),
-                in0=src.rearrange("p (n u e) -> p n u e", u=4 // run, e=run),
+                out=wide[group, g][:].rearrange("p u n e -> p n u e"),
+                in0=src.rearrange("p (n u e) -> p n u e", u=2, e=2),
                 scalar1=ones[:], scalar2=None, op0=ALU.mult)
 
-        def turn_x(G, g, u):
-            width = WIDTHS[G]
-            if single(G, g, u):
-                xbank[G, g, u] = psum.tile([P, 2 * width], BF16, name="xbank")
+        def turn_x(group, g, u):
+            if as_bf16(group, g, u):
+                xbank[group, g, u] = bank([P, 2 * WIDE], BF16)
                 for e in range(2):
-                    for i in range(width // P):
-                        nc.tensor.transpose(xbank[G, g, u][:, e * width + i * P : e * width + (i + 1) * P], wide[G, g][:, u, i * P : (i + 1) * P, e], ident16[:])
+                    for i in range(TILES):
+                        nc.tensor.transpose(xbank[group, g, u][:, e * WIDE + i * P : e * WIDE + (i + 1) * P],
+                                            wide[group, g][:, u, i * P : (i + 1) * P, e], ident16[:])
             else:
-                xbank[G, g, u] = psum.tile([P, width], F32, name="xbank")
-                src = wide[G, g][:].rearrange("p u n e -> p (u n e)").bitcast(F32)[:, u * width : (u + 1) * width]
-                for i in range(width // P):
-                    nc.tensor.transpose(xbank[G, g, u][:, i * P : (i + 1) * P], src[:, i * P : (i + 1) * P], ident32[:])
+                xbank[group, g, u] = bank([P, WIDE], F32)
+                words = wide[group, g][:].rearrange("p u n e -> p (u n e)").bitcast(F32)[:, u * WIDE : (u + 1) * WIDE]
+                for i in range(TILES):
+                    nc.tensor.transpose(xbank[group, g, u][:, i * P : (i + 1) * P], words[:, i * P : (i + 1) * P], ident32[:])
 
-        def affine(G, g, u):
-            width = WIDTHS[G]
-            if u == 0:
-                planes[G, g] = work.tile([P, 4, width], BF16, name="planes", bufs=3)
+        def scale_x(group, g, u):
+            if (group, g) not in xrows:
+                xrows[group, g] = work.tile([P, PACK, WIDE], BF16, name="xrows", bufs=3)
             for e in range(2):
                 t = 2 * u + e
-                if single(G, g, u):
-                    src = xbank[G, g, u][:, e * width : (e + 1) * width]
+                if as_bf16(group, g, u):
+                    src = xbank[group, g, u][:, e * WIDE : (e + 1) * WIDE]
                 else:
-                    src = xbank[G, g, u][:].bitcast(BF16).rearrange("p (n e) -> p e n", e=2)[:, e, :]
-                if on_vector(G, g, u):
-                    nc.vector.tensor_scalar(out=planes[G, g][:, t, :], in0=src,
-                                            scalar1=scale[:, g, t : t + 1], scalar2=mean32[:, g, t : t + 1], op0=ALU.mult, op1=ALU.add)
+                    src = xbank[group, g, u][:].bitcast(BF16).rearrange("p (n e) -> p e n", e=2)[:, e, :]
+                if on_vector(group, u):
+                    nc.vector.tensor_scalar(out=xrows[group, g][:, t, :], in0=src, scalar1=scale[:, g, t : t + 1],
+                                            scalar2=mean32[:, g, t : t + 1], op0=ALU.mult, op1=ALU.add)
                 else:
-                    nc.scalar.activation(out=planes[G, g][:, t, :], in_=src, func=ACT.Identity,
+                    nc.scalar.activation(out=xrows[group, g][:, t, :], in_=src, func=ACT.Identity,
                                          scale=scale[:, g, t : t + 1], bias=mean32[:, g, t : t + 1])
 
-        def weave(key, src, width, copy):
-            woven[key] = work.tile([P, width, 4], BF16, name="woven" + key[0], bufs=3 if key[0] == "x" else 4, align_bytes=64)
-            copy(out=woven[key][:].rearrange("p (c i) t -> p c t i", i=4), in_=src[:].rearrange("p t (c i) -> p c t i", i=4))
+        def weave(key, src, width, bufs, copy):
+            woven[key] = work.tile([P, width, PACK], BF16, name="woven" + key[0], bufs=bufs, align_bytes=64)
+            copy(out=woven[key][:].rearrange("p (c i) t -> p c t i", i=4), in_=src.rearrange("p t (c i) -> p c t i", i=4))
 
         def quantise(key, width):
             codes[key] = keep.tile([P, width], U32, name="codes_%s%d_%d" % key, align_bytes=64)
@@ -141,201 +163,153 @@ def tile_cox_frailty_survival_b15_kernel(tc, X_bytes, X_scale, mean, B, H0, frai
             nc.vector.quantize_mx(out=codes[key][:].bitcast(FP8X4), scales=scales[key][:],
                                   in_=woven[key][:].rearrange("p n t -> p (n t)"))
 
-        def weave_b(q, g):
-            weave(("b", q, g), braw[q // 2, g][:, :, (q % 2) * S : (q % 2 + 1) * S], S, nc.scalar.copy if (q, g) in ((1, 0), (1, 1), (1, 2), (2, 0), (2, 1), (3, 0), (3, 1),) else nc.vector.tensor_copy)
+        def weave_b(quarter, g, copy):
+            side, part = divmod(quarter, 2)
+            weave(("b", quarter, g), braw[side, g][:, :, part * NARROW : (part + 1) * NARROW], NARROW, 6, copy)
 
-        def quantise_b(q, g):
-            quantise(("b", q, g), S)
+        def quantise_b(quarter, g):
+            quantise(("b", quarter, g), NARROW)
 
-        def weave_x(G, g):
-            weave(("x", G, g), planes[G, g], WIDTHS[G], nc.vector.tensor_copy)
+        def weave_x(group, g):
+            weave(("x", group, g), xrows[group, g][:], WIDE, 3, nc.vector.tensor_copy)
 
-        def quantise_x(G, g):
-            quantise(("x", G, g), WIDTHS[G])
+        def quantise_x(group, g):
+            quantise(("x", group, g), WIDE)
 
-        def product(G, h, j, first, width):
-            per_bank = W // width
-            key = (G, h, j // per_bank, first)
-            if j % per_bank == 0:
-                acc[key] = psum.tile([P, per_bank, width], F32, name="acc")
+        def product(group, j):
+            acc = bank([P, WIDE], F32)
+            quarter, part = divmod(j, 2)
+            columns = slice(part * P, (part + 1) * P)
             for g in range(PASSES):
-                nc.tensor.matmul_mx(out=acc[key][:, j % per_bank, :],
-                                    lhsT=codes["b", 2 * h + j // 2, g][:, (j % 2) * P : (j % 2 + 1) * P].bitcast(FP8X4),
-                                    lhsT_scale=scales["b", 2 * h + j // 2, g][:, (j % 2) * P : (j % 2 + 1) * P],
-                                    rhs=codes["x", G, g][:, first : first + width].bitcast(FP8X4),
-                                    rhs_scale=scales["x", G, g][:, first : first + width], start=(g == 0), stop=(g == PASSES - 1))
+                nc.tensor.matmul_mx(out=acc[:],
+                                    lhsT=codes["b", quarter, g][:, columns].bitcast(FP8X4),
+                                    lhsT_scale=scales["b", quarter, g][:, columns],
+                                    rhs=codes["x", group, g][:].bitcast(FP8X4), rhs_scale=scales["x", group, g][:],
+                                    start=(g == 0), stop=(g == PASSES - 1))
+            hazard[group, j] = work.tile([P, WIDE], F32, name="hazard", bufs=2 * TILES)
+            nc.scalar.activation(out=hazard[group, j][:], in_=acc[:], func=ACT.Exp, bias=log_h0[:, j : j + 1])
 
-        def first_exp(G, h, j, first, width):
-            per_bank = W // width
-            tile = work.tile([P, width], F32, name="hazard", bufs=10)
-            for i in range(width // P):
-                hazard[G, h, j, first // P + i] = tile[:, i * P : (i + 1) * P]
-            nc.scalar.activation(out=tile[:], in_=acc[G, h, j // per_bank, first][:, j % per_bank, :], func=ACT.Exp,
-                                 bias=log_h0[:, 4 * h + j : 4 * h + j + 1])
+        def place(block):
+            group, side = divmod(block // TILES, SIDES)
+            return group, side, (block % TILES) * P
 
-        def turn_e(slab, r):
-            G, h, half = slab
-            ebank[slab, r] = psum.tile([P, W], F32, name="ebank", tag="acc" if slab == (len(WIDTHS) - 1, 1, 1) else "ebank")
-            for j in range(4):
-                nc.tensor.transpose(ebank[slab, r][:, j * P : (j + 1) * P], hazard[G, h, j, 2 * half + r], ident32[:])
-
-        def second_exp(slab, r):
-            G, h, half = slab
-            first = STARTS[G] + half * S
-            if r == 0:
-                y[slab] = work.tile([P, 2, W], F32, name="y", tag="slab", bufs=SLABS)
-            col = first // P + r
-            nc.scalar.activation(out=y[slab][:, r, :], in_=ebank[slab, r][:], func=ACT.Exp, scale=neg_f[:, col : col + 1])
-            if r == 1:
-                dst = out_0[first : first + S, h * W : (h + 1) * W]
+        def survive(block):
+            group, side, first = place(block)
+            hbank = bank([P, WIDE], F32)
+            for j in range(TILES):
+                nc.tensor.transpose(hbank[:, j * P : (j + 1) * P], hazard[group, side * TILES + j][:, first : first + P], ident32[:])
+            slab = [s for s in SLABS if s[0] <= block][-1]
+            start, count = slab
+            if block == start:
+                y[slab] = work.tile([P, count, WIDE], F32, name="y", tag="slab", bufs=BLOCKS // 2)
+            i = group * TILES + block % TILES
+            nc.scalar.activation(out=y[slab][:, block - start, :], in_=hbank[:], func=ACT.Exp, scale=neg_f[:, i : i + 1])
+            if block == start + count - 1:
+                dst = out_0[(i + 1 - count) * P : (i + 1) * P, side * WIDE : (side + 1) * WIDE]
                 nc.sync.dma_start(out=dst.rearrange("(i p) n -> p i n", p=P), in_=y[slab][:])
 
         def round_y(slab):
-            y16[slab] = work.tile([P, 2, S, 2], BF16, name="y16", bufs=3)
+            y16[slab] = work.tile([P, 2, slab[1] * P, 2], BF16, name="y16", bufs=PLANES_MOST)
             nc.vector.tensor_copy(out=y16[slab][:], in_=y[slab][:].rearrange("p i (q u e) -> p u (i q) e", u=2, e=2))
 
-        def turn_y(slab):
+        def turn_y(slab, copy):
             words = y16[slab][:].rearrange("p u n e -> p (u n e)").bitcast(F32)
-            ybank[slab] = psum.tile([P, W], F32, name="ybank")
-            for q in range(4):
-                nc.tensor.transpose(ybank[slab][:, q * P : (q + 1) * P], words[:, q * P : (q + 1) * P], ident32[:])
-
-        def empty_y(slab, copy):
-            ywoven[slab] = work.tile([P, S, 2], F32, name="ywoven", bufs=5, align_bytes=64)
-            copy(out=ywoven[slab][:], in_=ybank[slab][:].rearrange("p (u m) -> p m u", u=2))
+            ybank = bank([P, 2 * slab[1] * P], F32)
+            for b in range(2 * slab[1]):
+                nc.tensor.transpose(ybank[:, b * P : (b + 1) * P], words[:, b * P : (b + 1) * P], ident32[:])
+            ywoven[slab] = work.tile([P, slab[1] * P, 2], F32, name="ywoven", bufs=PLANES_MOST + 1, align_bytes=64)
+            copy(out=ywoven[slab][:], in_=ybank[:].rearrange("p (u m) -> p m u", u=2))
 
         def quantise_y(slab):
-            G, h, half = slab
-            first = STARTS[G] + half * S
-            if G not in yscales:
-                yscales[G] = work.tile([P, HALVES, WIDTHS[G]], U8, name="yscales", align_bytes=64)
-            ycodes = work.tile([P, S], U32, name="ycodes", bufs=4, align_bytes=64)
-            nc.vector.quantize_mx(out=ycodes[:].bitcast(FP8X4), scales=yscales[G][:, h, half * S : (half + 1) * S],
+            group, side, first = place(slab[0])
+            width = slab[1] * P
+            half, person = divmod(group * WIDE + first, T // 2)
+            if first == 0:
+                ycodes[group, side] = work.tile([P, WIDE], U32, name="ycodes", bufs=4, align_bytes=64)
+            nc.vector.quantize_mx(out=ycodes[group, side][:, first : first + width].bitcast(FP8X4),
+                                  scales=yscales[half][:, side, person : person + width],
                                   in_=ywoven[slab][:].rearrange("p m u -> p (m u)").bitcast(BF16))
-            words = out_1[h].rearrange("p m t -> p (m t)").bitcast(I32)
-            nc.sync.dma_start(out=words[:, first : first + S], in_=ycodes[:].bitcast(I32))
-            quantised.append(G)
-            if quantised.count(G) == HALVES * WIDTHS[G] // S:
+            if first + width < WIDE:
+                return
+            words = out_1[side].rearrange("p m t -> p (m t)").bitcast(I32)
+            nc.sync.dma_start(out=words[:, group * WIDE : (group + 1) * WIDE], in_=ycodes[group, side][:].bitcast(I32))
+            if side == SIDES - 1 and person + width == T // 2:
+                queue = nc.scalar if group == GROUPS - 1 else nc.sync
+                persons = slice(half * T // 2, (half + 1) * T // 2)
                 for q in range(4):
-                    dst = out_2[:, 4 * q : 4 * q + 4, STARTS[G] : STARTS[G] + WIDTHS[G]].rearrange("h r m -> r h m").bitcast(I32)
-                    nc.sync.dma_start(out=dst, in_=yscales[G][32 * q : 32 * q + 4, :, :].bitcast(I32))
+                    dst = out_2[:, 4 * q : 4 * q + 4, persons].rearrange("h r m -> r h m")
+                    queue.dma_start(out=dst.bitcast(I32), in_=yscales[half][32 * q : 32 * q + 4, :, :].bitcast(I32))
 
-        def half_x(G, g, u):
-            turn_x(G, g, u)
-            affine(G, g, u)
+        def turn_and_scale(group, g):
+            for u in (1, 0) if on_vector(group, 1) else (0, 1):
+                turn_x(group, g, u)
+                scale_x(group, g, u)
 
-        widen(0, 0)
-        half_x(0, 0, 0)
-        half_x(0, 0, 1)
-        weave_b(0, 0)
-        widen(0, 1)
-        half_x(0, 1, 0)
-        half_x(0, 1, 1)
-        quantise_b(0, 0)
-        widen(0, 2)
-        half_x(0, 2, 0)
-        half_x(0, 2, 1)
-        weave_x(0, 0)
-        weave_b(0, 1)
-        quantise_x(0, 0)
-        quantise_b(0, 1)
-        weave_x(0, 1)
-        weave_b(0, 2)
-        quantise_x(0, 1)
-        weave_x(0, 2)
-        quantise_b(0, 2)
+        windows = range(-1, ROUNDS + 2)
+        chunks = {w: [(group, g) for group in range(1, GROUPS) for g in range(PASSES) if window_of(group, g) == w]
+                  for w in range(-1, ROUNDS + 3)}
+        blocks = {w: [b for b in range(BLOCKS) if (b + LAG) // TILES == w] for w in windows}
+
+        planes, waiting = {}, list(SLABS)
+        for w in range(-1, ROUNDS + 3):
+            most = 0 if w < PLANES_FROM else 1 if w <= last_x_window or w == ROUNDS else PLANES_MOST
+            planes[w] = [s for s in waiting[:most] if (s[0] + s[1] - 1 + LAG) // TILES < w]
+            waiting = waiting[len(planes[w]) :]
+
+        def emptied_by(slab, w):
+            early, late = w <= last_x_window, place(slab[0])[0] == GROUPS - 1
+            return nc.scalar.copy if early or (late and slab != SLABS[-2]) else nc.vector.tensor_copy
+
         for g in range(PASSES):
-            if (1, g) in ((1, 0), (1, 1), (1, 2), (2, 0), (2, 1), (3, 0), (3, 1),):
-                weave_b(1, g)
-        quantise_x(0, 2)
-        widen(1, 0)
+            widen(0, g)
+            weave_b(1, g, nc.scalar.copy)
+            turn_and_scale(0, g)
+            if g == 0:
+                weave_b(0, g, nc.vector.tensor_copy)
+        for g in range(1, PASSES):
+            weave_b(0, g, nc.vector.tensor_copy)
+        widen(*chunks[-1][0])
+        for g in range(PASSES):
+            if g == PASSES - 1:
+                turn_and_scale(*chunks[-1][0])
+            quantise_b(0, g)
+            weave_x(0, g)
+            quantise_b(1, g)
+            quantise_x(0, g)
 
-        steps, slabs, ready = [], [], {}
-        for G, width in enumerate(WIDTHS):
-            for h in range(HALVES):
-                parts = width // S
-                if 2 * G + h >= 8 - 0:
-                    for half in range(parts):
-                        steps.append([(G, h, j, half * S, S) for j in range(4)])
-                        slabs.append((G, h, half))
-                        ready.setdefault(len(steps), []).append((G, h, half))
-                else:
-                    for part in range(parts):
-                        steps.append([(G, h, j, 0, width) for j in range(part * 4 // parts, (part + 1) * 4 // parts)])
-                    for half in range(parts):
-                        slabs.append((G, h, half))
-                        ready.setdefault(min(len(steps) + half, 16), []).append((G, h, half))
-        x_at = {0: [(1,0,0),(1,0,1)], 1: [(1,1,0),(1,1,1)], 2: [(1,2,0),(1,2,1)], 3: [(2,0,0),(2,0,1)], 4: [(2,1,0),(2,1,1)], 5: [(2,2,0),(2,2,1)], 6: [(3,0,0)], 7: [(3,0,1)], 8: [(3,1,0)], 9: [(3,1,1)], 10: [(3,2,0),(3,2,1)]}
-        b_at = {0: [(2, 0), (2, 1)], 1: [(2, 2), (3, 0), (3, 1)], 2: [(3, 2)], -1: [(1, 0), (1, 1), (1, 2)]}
-        y_at = {7: [0], 8: [1], 9: [2], 10: [3], 11: [4], 12: [5,6], 13: [7,8], 14: [9,10], 15: [11,12], 16: [13], 17: [14,15]}
-        ev_s = lambda step, r: step<12 or step>15
-        on_s = ((1, 0), (1, 1), (1, 2), (2, 0), (2, 1), (3, 0), (3, 1),)
-        for step in range(0, 22):
-            products = steps[step] if 0 <= step < len(steps) else []
-            es = [(s, r) for s in ready.get(step, []) for r in range(2)]
-            xs = x_at.get(step, [])
-            done = [(G, g) for G, g, u in x_at.get(step - 2, []) if u == 1 and not on_vector(G, g, u)]
-            done = done + [(G, g) for G, g, u in x_at.get(step - 1, []) if u == 1 and on_vector(G, g, u)]
-            ahead = [(G, g) for G, g, u in x_at.get(step + 1, []) if u == 0 and (G, g) not in wide]
-            ys = [slabs[s] for s in y_at.get(step, [])]
-            before = list(enumerate(y_at.get(step - 1, [])))
-            late = [slabs[s] for r, s in enumerate(y_at.get(step - 2, [])) if ev_s(step - 2, r)]
-            late = late + [slabs[s] for r, s in before if not ev_s(step - 1, r)]
-            bs = b_at.get(step, [])
-            for m in products:
-                product(*m)
-            for x in x_at.get(step - 1, []):
-                if on_vector(*x):
-                    affine(*x)
-            for r, s in before:
-                if not ev_s(step - 1, r):
-                    empty_y(slabs[s], nc.vector.tensor_copy)
-            for s in ys:
+        for w in windows:
+            if 0 <= w < ROUNDS:
+                group, side = divmod(w, SIDES)
+                for j in range(side * TILES, (side + 1) * TILES):
+                    product(group, j)
+
+            for b in blocks[w]:
+                if b // TILES < w:
+                    survive(b)
+            for s in planes[w]:
+                turn_y(s, emptied_by(s, w))
+            if w >= 0:
+                for chunk in chunks[w]:
+                    turn_and_scale(*chunk)
+            for b in blocks[w]:
+                if b // TILES == w:
+                    survive(b)
+
+            for s in planes[w + 1]:
                 round_y(s)
-            for c in ahead:
-                widen(*c)
-            for b in bs:
-                if b not in on_s:
-                    weave_b(*b)
-            for c in done:
-                weave_x(*c)
-            for b in b_at.get(step - 1, []):
-                if b in on_s:
-                    quantise_b(*b)
-            for b in bs:
-                if b not in on_s:
-                    quantise_b(*b)
-            for c in done:
-                quantise_x(*c)
-            for s in late:
+            for chunk in chunks[w + 1][:1]:
+                widen(*chunk)
+            for chunk in chunks[w]:
+                weave_x(*chunk)
+            for chunk in chunks[w + 1][1:]:
+                widen(*chunk)
+            for s in planes[w]:
                 quantise_y(s)
-
-            if len(es) > 2 and False:
-                for s in ys:
-                    turn_y(s)
-            for r in range(2):
-                if r < len(es):
-                    turn_e(*es[r])
-                if r < len(xs):
-                    turn_x(*xs[r])
-            if len(es) <= 2:
-                for s in ys:
-                    turn_y(s)
-            for m in products:
-                first_exp(*m)
-            for r in range(max(len(es), 2)):
-                if r < len(es):
-                    second_exp(*es[r])
-                if r < len(xs) and not on_vector(*xs[r]):
-                    affine(*xs[r])
-                if r + 2 < len(es):
-                    turn_e(*es[r + 2])
-            if len(es) > 2 and not False:
-                for s in ys:
-                    turn_y(s)
-            for b in bs:
-                if b in on_s:
-                    weave_b(*b)
-            for r in range(len(ys)):
-                if ev_s(step, r):
-                    empty_y(ys[r], nc.scalar.copy)
+            for chunk in chunks[w]:
+                quantise_x(*chunk)
+            if w == -1:
+                pieces = [(quarter, g) for quarter in (2, 3) for g in range(PASSES)]
+                for quarter, g in pieces:
+                    weave_b(quarter, g, nc.scalar.copy if g < PIECES_ON_SCALAR else nc.vector.tensor_copy)
+                for quarter, g in pieces:
+                    quantise_b(quarter, g)

@@ -25,14 +25,14 @@ GROUPS = T // WIDE
 SIDES = N // WIDE
 TILES = WIDE // P
 ROUNDS = GROUPS * SIDES
-BLOCKS = ROUNDS * TILES
+STRIPS = ROUNDS * TILES
 BANKS = 8
-SLABS = tuple((b, 2) for b in range(0, BLOCKS - 2, 2)) + ((BLOCKS - 2, 1), (BLOCKS - 1, 1))
+SLABS = tuple((b, 2) for b in range(0, STRIPS - 2, 2)) + ((STRIPS - 2, 1), (STRIPS - 1, 1))
 
 PIECES_ON_SCALAR = 2
-LAG = 2
-PLANES_FROM = 3
-PLANES_MOST = 4
+LEFT_OVER = 2
+PLANES_FIRST = 4
+PLANES_MOST = 6
 
 
 def tile_cox_frailty_survival_b15_kernel(tc, X_bytes, X_scale, mean, B, H0, frailty, out_0, out_1, out_2):
@@ -69,7 +69,7 @@ def tile_cox_frailty_survival_b15_kernel(tc, X_bytes, X_scale, mean, B, H0, frai
             nc.sync.dma_start(out=xbytes[group, g][:], in_=src.rearrange("(i p) k -> p i k", p=P))
 
         def load_b(side, g):
-            braw[side, g] = work.tile([P, PACK, WIDE], BF16, name="braw", tag="slab", bufs=BLOCKS // 2)
+            braw[side, g] = work.tile([P, PACK, WIDE], BF16, name="braw", tag="y", bufs=STRIPS // 2)
             src = B[g * WIDE : (g + 1) * WIDE, side * WIDE : (side + 1) * WIDE]
             nc.sync.dma_start(out=braw[side, g][:], in_=src.rearrange("(p t) n -> p t n", t=PACK))
 
@@ -94,27 +94,27 @@ def tile_cox_frailty_survival_b15_kernel(tc, X_bytes, X_scale, mean, B, H0, frai
         nc.tensor.transpose(cols[:], rows[:], ident16[:])
         log_h0 = keep.tile([P, N // P], F32, name="log_h0")
         nc.scalar.activation(out=log_h0[:], in_=cols[:, h0_rows], func=ACT.Ln)
-        warm = keep.tile([P, 1], F32, name="warm")
-        nc.scalar.activation(out=warm[:], in_=ones[:], func=ACT.Exp)
         neg_f = keep.tile([P, T // P], F32, name="neg_f")
         nc.scalar.activation(out=neg_f[:], in_=cols[:, f_rows], func=ACT.Copy, scale=-1.0)
+        warm = keep.tile([P, 1], F32, name="warm")
+        nc.scalar.activation(out=warm[:], in_=ones[:], func=ACT.Exp)
         mean32 = keep.tile([P, PASSES, PACK], F32, name="mean32")
         nc.scalar.copy(out=mean32[:], in_=mean16[:])
 
         wide, xbank, xrows, woven, codes, scales = {}, {}, {}, {}, {}, {}
         hazard, y, y16, ywoven, ycodes = {}, {}, {}, {}, {}
-        yscales = [keep.tile([P, SIDES, T // 2], U8, name="yscales%d" % half, align_bytes=64) for half in range(2)]
+        yscales = [keep.tile([P, SIDES, 2 * WIDE], U8, name="yscales%d" % n, align_bytes=64) for n in range(GROUPS // 2)]
 
         def window_of(group, g):
             return 2 * group - 3 + min(g, 1)
 
         last_x_window = window_of(GROUPS - 1, PASSES - 1)
 
-        def on_vector(group, u):
-            return group > 0 and u == 1
+        def on_vector(group, g, u):
+            return group > 0 and (u == 1 or (g == 0 and group % 2 == 1))
 
         def as_bf16(group, g, u):
-            return on_vector(group, u) and window_of(group, g) < last_x_window
+            return on_vector(group, g, u) and window_of(group, g) < last_x_window
 
         def widen(group, g):
             wide[group, g] = work.tile([P, 2, WIDE, 2], BF16, name="wide", bufs=3)
@@ -146,12 +146,12 @@ def tile_cox_frailty_survival_b15_kernel(tc, X_bytes, X_scale, mean, B, H0, frai
                     src = xbank[group, g, u][:, e * WIDE : (e + 1) * WIDE]
                 else:
                     src = xbank[group, g, u][:].bitcast(BF16).rearrange("p (n e) -> p e n", e=2)[:, e, :]
-                if on_vector(group, u):
+                if on_vector(group, g, u):
                     nc.vector.tensor_scalar(out=xrows[group, g][:, t, :], in0=src, scalar1=scale[:, g, t : t + 1],
                                             scalar2=mean32[:, g, t : t + 1], op0=ALU.mult, op1=ALU.add)
                 else:
                     nc.scalar.activation(out=xrows[group, g][:, t, :], in_=src, func=ACT.Identity,
-                                         scale=scale[:, g, t : t + 1], bias=mean32[:, g, t : t + 1])
+                                         scale=scale[:, g, t : t + 1], bias=mean16[:, g, t : t + 1])
 
         def weave(key, src, width, bufs, copy):
             woven[key] = work.tile([P, width, PACK], BF16, name="woven" + key[0], bufs=bufs, align_bytes=64)
@@ -165,7 +165,7 @@ def tile_cox_frailty_survival_b15_kernel(tc, X_bytes, X_scale, mean, B, H0, frai
 
         def weave_b(quarter, g, copy):
             side, part = divmod(quarter, 2)
-            weave(("b", quarter, g), braw[side, g][:, :, part * NARROW : (part + 1) * NARROW], NARROW, 6, copy)
+            weave(("b", quarter, g), braw[side, g][:, :, part * NARROW : (part + 1) * NARROW], NARROW, PLANES_MOST, copy)
 
         def quantise_b(quarter, g):
             quantise(("b", quarter, g), NARROW)
@@ -189,28 +189,29 @@ def tile_cox_frailty_survival_b15_kernel(tc, X_bytes, X_scale, mean, B, H0, frai
             hazard[group, j] = work.tile([P, WIDE], F32, name="hazard", bufs=2 * TILES)
             nc.scalar.activation(out=hazard[group, j][:], in_=acc[:], func=ACT.Exp, bias=log_h0[:, j : j + 1])
 
-        def place(block):
-            group, side = divmod(block // TILES, SIDES)
-            return group, side, (block % TILES) * P
+        def place(strip):
+            group, side = divmod(strip // TILES, SIDES)
+            return group, side, (strip % TILES) * P
 
-        def survive(block):
-            group, side, first = place(block)
+        def survive(strip):
+            group, side, first = place(strip)
             hbank = bank([P, WIDE], F32)
             for j in range(TILES):
                 nc.tensor.transpose(hbank[:, j * P : (j + 1) * P], hazard[group, side * TILES + j][:, first : first + P], ident32[:])
-            slab = [s for s in SLABS if s[0] <= block][-1]
-            start, count = slab
-            if block == start:
-                y[slab] = work.tile([P, count, WIDE], F32, name="y", tag="slab", bufs=BLOCKS // 2)
-            i = group * TILES + block % TILES
-            nc.scalar.activation(out=y[slab][:, block - start, :], in_=hbank[:], func=ACT.Exp, scale=neg_f[:, i : i + 1])
-            if block == start + count - 1:
-                dst = out_0[(i + 1 - count) * P : (i + 1) * P, side * WIDE : (side + 1) * WIDE]
-                nc.sync.dma_start(out=dst.rearrange("(i p) n -> p i n", p=P), in_=y[slab][:])
+            tile, r = divmod(strip, 2)
+            if r == 0:
+                y[tile] = work.tile([P, 2, WIDE], F32, name="y", bufs=STRIPS // 2)
+            i = group * TILES + strip % TILES
+            nc.scalar.activation(out=y[tile][:, r, :], in_=hbank[:], func=ACT.Exp, scale=neg_f[:, i : i + 1])
+            if r == 1:
+                dst = out_0[(i - 1) * P : (i + 1) * P, side * WIDE : (side + 1) * WIDE]
+                nc.sync.dma_start(out=dst.rearrange("(i p) n -> p i n", p=P), in_=y[tile][:])
 
         def round_y(slab):
-            y16[slab] = work.tile([P, 2, slab[1] * P, 2], BF16, name="y16", bufs=PLANES_MOST)
-            nc.vector.tensor_copy(out=y16[slab][:], in_=y[slab][:].rearrange("p i (q u e) -> p u (i q) e", u=2, e=2))
+            y16[slab] = work.tile([P, 2, slab[1] * P, 2], BF16, name="y16", tag="wovenb", bufs=PLANES_MOST, align_bytes=64)
+            tile, r = divmod(slab[0], 2)
+            src = y[tile][:, r : r + slab[1], :]
+            nc.vector.tensor_copy(out=y16[slab][:], in_=src.rearrange("m i (p u e) -> m u (i p) e", u=2, e=2))
 
         def turn_y(slab, copy):
             words = y16[slab][:].rearrange("p u n e -> p (u n e)").bitcast(F32)
@@ -223,47 +224,55 @@ def tile_cox_frailty_survival_b15_kernel(tc, X_bytes, X_scale, mean, B, H0, frai
         def quantise_y(slab):
             group, side, first = place(slab[0])
             width = slab[1] * P
-            half, person = divmod(group * WIDE + first, T // 2)
+            pair, person = divmod(group * WIDE + first, 2 * WIDE)
             if first == 0:
                 ycodes[group, side] = work.tile([P, WIDE], U32, name="ycodes", bufs=4, align_bytes=64)
             nc.vector.quantize_mx(out=ycodes[group, side][:, first : first + width].bitcast(FP8X4),
-                                  scales=yscales[half][:, side, person : person + width],
+                                  scales=yscales[pair][:, side, person : person + width],
                                   in_=ywoven[slab][:].rearrange("p m u -> p (m u)").bitcast(BF16))
             if first + width < WIDE:
                 return
             words = out_1[side].rearrange("p m t -> p (m t)").bitcast(I32)
             nc.sync.dma_start(out=words[:, group * WIDE : (group + 1) * WIDE], in_=ycodes[group, side][:].bitcast(I32))
-            if side == SIDES - 1 and person + width == T // 2:
+            if side == SIDES - 1 and person + width == 2 * WIDE:
                 queue = nc.scalar if group == GROUPS - 1 else nc.sync
-                persons = slice(half * T // 2, (half + 1) * T // 2)
-                for q in range(4):
-                    dst = out_2[:, 4 * q : 4 * q + 4, persons].rearrange("h r m -> r h m")
-                    queue.dma_start(out=dst.bitcast(I32), in_=yscales[half][32 * q : 32 * q + 4, :, :].bitcast(I32))
+                persons = slice(pair * 2 * WIDE, (pair + 1) * 2 * WIDE)
+                for a in range(4):
+                    dst = out_2[:, 4 * a : 4 * a + 4, persons].rearrange("h r m -> r h m")
+                    queue.dma_start(out=dst.bitcast(I32), in_=yscales[pair][32 * a : 32 * a + 4, :, :].bitcast(I32))
 
         def turn_and_scale(group, g):
-            for u in (1, 0) if on_vector(group, 1) else (0, 1):
+            for u in (1, 0) if on_vector(group, g, 1) else (0, 1):
                 turn_x(group, g, u)
                 scale_x(group, g, u)
 
         windows = range(-1, ROUNDS + 2)
         chunks = {w: [(group, g) for group in range(1, GROUPS) for g in range(PASSES) if window_of(group, g) == w]
                   for w in range(-1, ROUNDS + 3)}
-        blocks = {w: [b for b in range(BLOCKS) if (b + LAG) // TILES == w] for w in windows}
+
+        def strip_window(strip):
+            w, i = divmod(strip, TILES)
+            return w + 1 if w % SIDES == 0 and i >= TILES - LEFT_OVER else w
+
+        strips = {w: [b for b in range(STRIPS) if strip_window(b) == w] for w in windows}
 
         planes, waiting = {}, list(SLABS)
         for w in range(-1, ROUNDS + 3):
-            most = 0 if w < PLANES_FROM else 1 if w <= last_x_window or w == ROUNDS else PLANES_MOST
-            planes[w] = [s for s in waiting[:most] if (s[0] + s[1] - 1 + LAG) // TILES < w]
+            most = {last_x_window + 1: PLANES_FIRST, ROUNDS: 1}.get(w, PLANES_MOST if w > last_x_window else 0)
+            planes[w] = [s for s in waiting[:most] if strip_window(s[0] + s[1] - 1) < w]
             waiting = waiting[len(planes[w]) :]
 
         def emptied_by(slab, w):
-            early, late = w <= last_x_window, place(slab[0])[0] == GROUPS - 1
-            return nc.scalar.copy if early or (late and slab != SLABS[-2]) else nc.vector.tensor_copy
+            if w < ROUNDS - 1:
+                on_scalar = planes[w].index(slab) < len(planes[w]) // 2
+            else:
+                on_scalar = place(slab[0])[0] == GROUPS - 1 and slab != SLABS[-2]
+            return nc.scalar.copy if on_scalar else nc.vector.tensor_copy
 
         for g in range(PASSES):
             widen(0, g)
-            weave_b(1, g, nc.scalar.copy)
             turn_and_scale(0, g)
+            weave_b(1, g, nc.scalar.copy)
             if g == 0:
                 weave_b(0, g, nc.vector.tensor_copy)
         for g in range(1, PASSES):
@@ -283,7 +292,7 @@ def tile_cox_frailty_survival_b15_kernel(tc, X_bytes, X_scale, mean, B, H0, frai
                 for j in range(side * TILES, (side + 1) * TILES):
                     product(group, j)
 
-            for b in blocks[w]:
+            for b in strips[w]:
                 if b // TILES < w:
                     survive(b)
             for s in planes[w]:
@@ -291,7 +300,7 @@ def tile_cox_frailty_survival_b15_kernel(tc, X_bytes, X_scale, mean, B, H0, frai
             if w >= 0:
                 for chunk in chunks[w]:
                     turn_and_scale(*chunk)
-            for b in blocks[w]:
+            for b in strips[w]:
                 if b // TILES == w:
                     survive(b)
 

from contextlib import ExitStack

import concourse.mybir as mybir
from concourse.masks import make_identity

T, K, N = 2048, 1536, 1024
FLOPS = 2 * T * K * N

F32 = mybir.dt.float32
BF16 = mybir.dt.bfloat16
U32 = mybir.dt.uint32
I32 = mybir.dt.int32
U8 = mybir.dt.uint8
FP8 = mybir.dt.float8_e4m3fn
FP8X4 = mybir.dt.float8_e4m3fn_x4
ALU = mybir.AluOpType
ACT = mybir.ActivationFunctionType

P = 128
PACK = 4
WIDE = 512
NARROW = 256
PASSES = K // WIDE
GROUPS = T // WIDE
SIDES = N // WIDE
TILES = WIDE // P
ROUNDS = GROUPS * SIDES
STRIPS = ROUNDS * TILES
BANKS = 8
SLABS = tuple((b, 2) for b in range(0, STRIPS - 2, 2)) + ((STRIPS - 2, 1), (STRIPS - 1, 1))

PIECES_ON_SCALAR = 2
LEFT_OVER = 2
PLANES_FIRST = 4
PLANES_MOST = 6


def tile_cox_frailty_survival_b15_kernel(tc, X_bytes, X_scale, mean, B, H0, frailty, out_0, out_1, out_2):
    nc = tc.nc
    with ExitStack() as ctx:
        keep = ctx.enter_context(tc.tile_pool(name="keep", bufs=1))
        work = ctx.enter_context(tc.tile_pool(name="work", bufs=2))
        psum = ctx.enter_context(tc.psum_pool(name="psum", bufs=BANKS))
        ctx.enter_context(tc.manual_schedule())

        def bank(shape, dtype):
            return psum.tile(shape, dtype, name="bank")

        rows = keep.tile([P, P], BF16, name="rows")
        nc.gpsimd.memset(rows[:], 0.0)
        ones = keep.tile([P, 1], F32, name="ones")
        nc.gpsimd.memset(ones[:], 1.0)
        ident16 = keep.tile([P, P], BF16, name="ident16")
        make_identity(nc, ident16[:])
        ident32 = keep.tile([P, P], F32, name="ident32")
        make_identity(nc, ident32[:])

        h0_rows, f_rows = slice(0, N // P), slice(N // P, N // P + T // P)
        scale = keep.tile([P, PASSES, PACK], F32, name="scale")
        mean16 = keep.tile([P, PASSES, PACK], BF16, name="mean16")
        nc.scalar.dma_start(out=scale[:], in_=X_scale.rearrange("o (g p t) -> p (o g) t", p=P, t=PACK))
        nc.scalar.dma_start(out=mean16[:], in_=mean.rearrange("o (g p t) -> p (o g) t", p=P, t=PACK))

        xbytes, braw = {}, {}

        def load_x(group, g):
            xbytes[group, g] = keep.tile([P, TILES, WIDE], U8, name="xbytes%d_%d" % (group, g))
            src = X_bytes[group * WIDE : (group + 1) * WIDE, g * WIDE : (g + 1) * WIDE]
            nc.sync.dma_start(out=xbytes[group, g][:], in_=src.rearrange("(i p) k -> p i k", p=P))

        def load_b(side, g):
            braw[side, g] = work.tile([P, PACK, WIDE], BF16, name="braw", tag="y", bufs=STRIPS // 2)
            src = B[g * WIDE : (g + 1) * WIDE, side * WIDE : (side + 1) * WIDE]
            nc.sync.dma_start(out=braw[side, g][:], in_=src.rearrange("(p t) n -> p t n", t=PACK))

        load_x(0, 0)
        nc.sync.dma_start(out=rows[h0_rows, :], in_=H0.rearrange("o (j p) -> (o j) p", p=P))
        nc.sync.dma_start(out=rows[f_rows, :], in_=frailty.rearrange("(i p) o -> i (p o)", p=P))
        load_b(0, 0)
        load_x(0, 1)
        load_x(0, 2)
        load_b(0, 1)
        load_b(0, 2)
        load_x(1, 0)
        load_x(1, 1)
        for g in range(PASSES):
            load_b(1, g)
        load_x(1, 2)
        for group in range(2, GROUPS):
            for g in range(PASSES):
                load_x(group, g)

        cols = bank([P, P], BF16)
        nc.tensor.transpose(cols[:], rows[:], ident16[:])
        log_h0 = keep.tile([P, N // P], F32, name="log_h0")
        nc.scalar.activation(out=log_h0[:], in_=cols[:, h0_rows], func=ACT.Ln)
        neg_f = keep.tile([P, T // P], F32, name="neg_f")
        nc.scalar.activation(out=neg_f[:], in_=cols[:, f_rows], func=ACT.Copy, scale=-1.0)
        warm = keep.tile([P, 1], F32, name="warm")
        nc.scalar.activation(out=warm[:], in_=ones[:], func=ACT.Exp)
        mean32 = keep.tile([P, PASSES, PACK], F32, name="mean32")
        nc.scalar.copy(out=mean32[:], in_=mean16[:])

        wide, xbank, xrows, woven, codes, scales = {}, {}, {}, {}, {}, {}
        hazard, y, y16, ywoven, ycodes = {}, {}, {}, {}, {}
        yscales = [keep.tile([P, SIDES, 2 * WIDE], U8, name="yscales%d" % n, align_bytes=64) for n in range(GROUPS // 2)]

        def window_of(group, g):
            return 2 * group - 3 + min(g, 1)

        last_x_window = window_of(GROUPS - 1, PASSES - 1)

        def on_vector(group, g, u):
            return group > 0 and (u == 1 or (g == 0 and group % 2 == 1))

        def as_bf16(group, g, u):
            return on_vector(group, g, u) and window_of(group, g) < last_x_window

        def widen(group, g):
            wide[group, g] = work.tile([P, 2, WIDE, 2], BF16, name="wide", bufs=3)
            src = xbytes[group, g][:].rearrange("p i k -> p (i k)").bitcast(FP8)
            nc.vector.tensor_scalar(
                out=wide[group, g][:].rearrange("p u n e -> p n u e"),
                in0=src.rearrange("p (n u e) -> p n u e", u=2, e=2),
                scalar1=ones[:], scalar2=None, op0=ALU.mult)

        def turn_x(group, g, u):
            if as_bf16(group, g, u):
                xbank[group, g, u] = bank([P, 2 * WIDE], BF16)
                for e in range(2):
                    for i in range(TILES):
                        nc.tensor.transpose(xbank[group, g, u][:, e * WIDE + i * P : e * WIDE + (i + 1) * P],
                                            wide[group, g][:, u, i * P : (i + 1) * P, e], ident16[:])
            else:
                xbank[group, g, u] = bank([P, WIDE], F32)
                words = wide[group, g][:].rearrange("p u n e -> p (u n e)").bitcast(F32)[:, u * WIDE : (u + 1) * WIDE]
                for i in range(TILES):
                    nc.tensor.transpose(xbank[group, g, u][:, i * P : (i + 1) * P], words[:, i * P : (i + 1) * P], ident32[:])

        def scale_x(group, g, u):
            if (group, g) not in xrows:
                xrows[group, g] = work.tile([P, PACK, WIDE], BF16, name="xrows", bufs=3)
            for e in range(2):
                t = 2 * u + e
                if as_bf16(group, g, u):
                    src = xbank[group, g, u][:, e * WIDE : (e + 1) * WIDE]
                else:
                    src = xbank[group, g, u][:].bitcast(BF16).rearrange("p (n e) -> p e n", e=2)[:, e, :]
                if on_vector(group, g, u):
                    nc.vector.tensor_scalar(out=xrows[group, g][:, t, :], in0=src, scalar1=scale[:, g, t : t + 1],
                                            scalar2=mean32[:, g, t : t + 1], op0=ALU.mult, op1=ALU.add)
                else:
                    nc.scalar.activation(out=xrows[group, g][:, t, :], in_=src, func=ACT.Identity,
                                         scale=scale[:, g, t : t + 1], bias=mean16[:, g, t : t + 1])

        def weave(key, src, width, bufs, copy):
            woven[key] = work.tile([P, width, PACK], BF16, name="woven" + key[0], bufs=bufs, align_bytes=64)
            copy(out=woven[key][:].rearrange("p (c i) t -> p c t i", i=4), in_=src.rearrange("p t (c i) -> p c t i", i=4))

        def quantise(key, width):
            codes[key] = keep.tile([P, width], U32, name="codes_%s%d_%d" % key, align_bytes=64)
            scales[key] = keep.tile([P, width], U8, name="scales_%s%d_%d" % key, align_bytes=64)
            nc.vector.quantize_mx(out=codes[key][:].bitcast(FP8X4), scales=scales[key][:],
                                  in_=woven[key][:].rearrange("p n t -> p (n t)"))

        def weave_b(quarter, g, copy):
            side, part = divmod(quarter, 2)
            weave(("b", quarter, g), braw[side, g][:, :, part * NARROW : (part + 1) * NARROW], NARROW, PLANES_MOST, copy)

        def quantise_b(quarter, g):
            quantise(("b", quarter, g), NARROW)

        def weave_x(group, g):
            weave(("x", group, g), xrows[group, g][:], WIDE, 3, nc.vector.tensor_copy)

        def quantise_x(group, g):
            quantise(("x", group, g), WIDE)

        def product(group, j):
            acc = bank([P, WIDE], F32)
            quarter, part = divmod(j, 2)
            columns = slice(part * P, (part + 1) * P)
            for g in range(PASSES):
                nc.tensor.matmul_mx(out=acc[:],
                                    lhsT=codes["b", quarter, g][:, columns].bitcast(FP8X4),
                                    lhsT_scale=scales["b", quarter, g][:, columns],
                                    rhs=codes["x", group, g][:].bitcast(FP8X4), rhs_scale=scales["x", group, g][:],
                                    start=(g == 0), stop=(g == PASSES - 1))
            hazard[group, j] = work.tile([P, WIDE], F32, name="hazard", bufs=2 * TILES)
            nc.scalar.activation(out=hazard[group, j][:], in_=acc[:], func=ACT.Exp, bias=log_h0[:, j : j + 1])

        def place(strip):
            group, side = divmod(strip // TILES, SIDES)
            return group, side, (strip % TILES) * P

        def survive(strip):
            group, side, first = place(strip)
            hbank = bank([P, WIDE], F32)
            for j in range(TILES):
                nc.tensor.transpose(hbank[:, j * P : (j + 1) * P], hazard[group, side * TILES + j][:, first : first + P], ident32[:])
            tile, r = divmod(strip, 2)
            if r == 0:
                y[tile] = work.tile([P, 2, WIDE], F32, name="y", bufs=STRIPS // 2)
            i = group * TILES + strip % TILES
            nc.scalar.activation(out=y[tile][:, r, :], in_=hbank[:], func=ACT.Exp, scale=neg_f[:, i : i + 1])
            if r == 1:
                dst = out_0[(i - 1) * P : (i + 1) * P, side * WIDE : (side + 1) * WIDE]
                nc.sync.dma_start(out=dst.rearrange("(i p) n -> p i n", p=P), in_=y[tile][:])

        def round_y(slab):
            y16[slab] = work.tile([P, 2, slab[1] * P, 2], BF16, name="y16", tag="wovenb", bufs=PLANES_MOST, align_bytes=64)
            tile, r = divmod(slab[0], 2)
            src = y[tile][:, r : r + slab[1], :]
            nc.vector.tensor_copy(out=y16[slab][:], in_=src.rearrange("m i (p u e) -> m u (i p) e", u=2, e=2))

        def turn_y(slab, copy):
            words = y16[slab][:].rearrange("p u n e -> p (u n e)").bitcast(F32)
            ybank = bank([P, 2 * slab[1] * P], F32)
            for b in range(2 * slab[1]):
                nc.tensor.transpose(ybank[:, b * P : (b + 1) * P], words[:, b * P : (b + 1) * P], ident32[:])
            ywoven[slab] = work.tile([P, slab[1] * P, 2], F32, name="ywoven", bufs=PLANES_MOST + 1, align_bytes=64)
            copy(out=ywoven[slab][:], in_=ybank[:].rearrange("p (u m) -> p m u", u=2))

        def quantise_y(slab):
            group, side, first = place(slab[0])
            width = slab[1] * P
            pair, person = divmod(group * WIDE + first, 2 * WIDE)
            if first == 0:
                ycodes[group, side] = work.tile([P, WIDE], U32, name="ycodes", bufs=4, align_bytes=64)
            nc.vector.quantize_mx(out=ycodes[group, side][:, first : first + width].bitcast(FP8X4),
                                  scales=yscales[pair][:, side, person : person + width],
                                  in_=ywoven[slab][:].rearrange("p m u -> p (m u)").bitcast(BF16))
            if first + width < WIDE:
                return
            words = out_1[side].rearrange("p m t -> p (m t)").bitcast(I32)
            nc.sync.dma_start(out=words[:, group * WIDE : (group + 1) * WIDE], in_=ycodes[group, side][:].bitcast(I32))
            if side == SIDES - 1 and person + width == 2 * WIDE:
                queue = nc.scalar if group == GROUPS - 1 else nc.sync
                persons = slice(pair * 2 * WIDE, (pair + 1) * 2 * WIDE)
                for a in range(4):
                    dst = out_2[:, 4 * a : 4 * a + 4, persons].rearrange("h r m -> r h m")
                    queue.dma_start(out=dst.bitcast(I32), in_=yscales[pair][32 * a : 32 * a + 4, :, :].bitcast(I32))

        def turn_and_scale(group, g):
            for u in (1, 0) if on_vector(group, g, 1) else (0, 1):
                turn_x(group, g, u)
                scale_x(group, g, u)

        windows = range(-1, ROUNDS + 2)
        chunks = {w: [(group, g) for group in range(1, GROUPS) for g in range(PASSES) if window_of(group, g) == w]
                  for w in range(-1, ROUNDS + 3)}

        def strip_window(strip):
            w, i = divmod(strip, TILES)
            return w + 1 if w % SIDES == 0 and i >= TILES - LEFT_OVER else w

        strips = {w: [b for b in range(STRIPS) if strip_window(b) == w] for w in windows}

        planes, waiting = {}, list(SLABS)
        for w in range(-1, ROUNDS + 3):
            most = {last_x_window + 1: PLANES_FIRST, ROUNDS: 1}.get(w, PLANES_MOST if w > last_x_window else 0)
            planes[w] = [s for s in waiting[:most] if strip_window(s[0] + s[1] - 1) < w]
            waiting = waiting[len(planes[w]) :]

        def emptied_by(slab, w):
            if w < ROUNDS - 1:
                on_scalar = planes[w].index(slab) < len(planes[w]) // 2
            else:
                on_scalar = place(slab[0])[0] == GROUPS - 1 and slab != SLABS[-2]
            return nc.scalar.copy if on_scalar else nc.vector.tensor_copy

        for g in range(PASSES):
            widen(0, g)
            turn_and_scale(0, g)
            weave_b(1, g, nc.scalar.copy)
            if g == 0:
                weave_b(0, g, nc.vector.tensor_copy)
        for g in range(1, PASSES):
            weave_b(0, g, nc.vector.tensor_copy)
        widen(*chunks[-1][0])
        for g in range(PASSES):
            if g == PASSES - 1:
                turn_and_scale(*chunks[-1][0])
            quantise_b(0, g)
            weave_x(0, g)
            quantise_b(1, g)
            quantise_x(0, g)

        for w in windows:
            if 0 <= w < ROUNDS:
                group, side = divmod(w, SIDES)
                for j in range(side * TILES, (side + 1) * TILES):
                    product(group, j)

            for b in strips[w]:
                if b // TILES < w:
                    survive(b)
            for s in planes[w]:
                turn_y(s, emptied_by(s, w))
            if w >= 0:
                for chunk in chunks[w]:
                    turn_and_scale(*chunk)
            for b in strips[w]:
                if b // TILES == w:
                    survive(b)

            for s in planes[w + 1]:
                round_y(s)
            for chunk in chunks[w + 1][:1]:
                widen(*chunk)
            for chunk in chunks[w]:
                weave_x(*chunk)
            for chunk in chunks[w + 1][1:]:
                widen(*chunk)
            for s in planes[w]:
                quantise_y(s)
            for chunk in chunks[w]:
                quantise_x(*chunk)
            if w == -1:
                pieces = [(quarter, g) for quarter in (2, 3) for g in range(PASSES)]
                for quarter, g in pieces:
                    weave_b(quarter, g, nc.scalar.copy if g < PIECES_ON_SCALAR else nc.vector.tensor_copy)
                for quarter, g in pieces:
                    quantise_b(quarter, g)
